import numpy as np
import ml_dtypes


def mxq(x, axis, fmt="e4m3"):
    dtype, down = {"e4m3": (ml_dtypes.float8_e4m3fn, 7), "e5m2": (ml_dtypes.float8_e5m2, 14)}[fmt]
    v = np.moveaxis(np.asarray(x, np.float32).astype(ml_dtypes.bfloat16).astype(np.float64), axis, -1)
    blocks = v.reshape(v.shape[:-1] + (-1, 32))
    amax = np.abs(blocks).max(-1, keepdims=True)
    byte = np.maximum(np.where(amax > 0, np.frexp(amax)[1] - 1 + 127, 0) - down, 1)
    scale = np.exp2(byte - 127.0)
    codes = (blocks / scale).astype(np.float32).astype(dtype).astype(np.float64)
    return np.moveaxis((codes * scale).reshape(v.shape), -1, axis)


WIDE = False


def mx_kscale(k):
    if not WIDE:
        return np.ones(k)
    levels = np.array([10, -10, 5, -5, 0])
    if k % 512:
        return np.exp2(np.random.permutation(np.resize(levels, k // 32))).repeat(32)
    a = np.empty((k // 512, 16))
    for p in range(k // 512):
        a[p, :8] = np.random.permutation(np.resize(levels, 8))
        for g in range(8):
            far = levels[np.abs(levels - a[p, g]) >= 10]
            a[p, g + 8] = far[np.random.randint(len(far))]
    return np.exp2(a.ravel()).repeat(32)


def f64(x):
    return np.asarray(x).astype(np.float64)


def striped(idx):
    return np.tile(idx.reshape(-1, 16).T, (8, 1)).astype(np.uint16)


def unstriped(offs):
    return offs[:16].T.reshape(-1).astype(np.int64)


def pack_weight(w):
    k, n = w.shape
    w = f64(np.asarray(w, np.float32).astype(ml_dtypes.bfloat16)).reshape(k // 32, 32, n)
    amax = np.abs(w).max(1)
    byte = np.clip(np.where(amax > 0, np.frexp(amax)[1] - 1 + 127 - 7, 1), 1, 254)
    scaled = (w * np.exp2(127.0 - byte)[:, None, :]).reshape(k, n).astype(np.float32)
    words = np.ascontiguousarray(scaled.reshape(k // 512, 128, 4, n).transpose(0, 1, 3, 2)).astype(ml_dtypes.float8_e4m3fn).view(np.uint8)
    return words, np.ascontiguousarray(byte.astype(np.uint8).reshape(k // 512, 16, n))


def unpack_weight(words, scales):
    g, p, n, _ = words.shape
    vals = np.ascontiguousarray(words).view(ml_dtypes.float8_e4m3fn).astype(np.float64) * np.repeat(np.exp2(scales.astype(np.float64) - 127.0), 8, axis=1)[..., None]
    return vals.transpose(0, 1, 3, 2).reshape(g * 512, n)


def sigmoid(v):
    return 1.0 / (1.0 + np.exp(-np.maximum(v, -700.0)))


K, T, S, H, V = 1024, 2048, 512, 512, 512


def setup_inputs():
    n = np.random.standard_normal
    s = mx_kscale(K)[:, None]
    u = mx_kscale(H)
    packed_xT = pack_weight(n((K, T)) * s)
    return {
        "x_words": packed_xT[0],
        "x_scales": packed_xT[1],
        "w1": (n((K, H)) / np.sqrt(K) / s).astype(np.float32),
        "unit": (np.random.uniform(0.7, 1.3, (H, 1)) * u[:, None]).astype(np.float32),
        "inv": (np.random.uniform(0.7, 1.3, (H, 1)) / u[:, None] / np.sqrt(H)).astype(np.float32),
        "sim": ((np.random.uniform(size=(S, V)) < 0.2) * 1.0).astype(np.float32),
        "wt": (np.random.uniform(0.5, 2.0, (S, V))).astype(np.float32),
        "offs": striped(np.random.permutation(T)[:S]),
        "other": striped(np.random.permutation(T)[:V]),
    }


def reference(x_words, x_scales, w1, unit, inv, sim, wt, offs, other):
    xq = unpack_weight(x_words, x_scales)[:, unstriped(offs)]
    w1q = mxq(f64(w1), 0, "e4m3")
    ha = f64(unit) * (np.tanh(2.0 * (w1q.T @ xq)))
    x_other = unpack_weight(x_words, x_scales)[:, unstriped(other)]
    hb = f64(inv) * (np.tanh(2.0 * (w1q.T @ x_other)))
    y = mxq(ha, 0, "e4m3").T @ mxq(hb, 0, "e4m3")
    return f64(wt) * (sigmoid(y) - f64(sim))

@@ -1,0 +1,262 @@
+from contextlib import ExitStack
+
+import concourse.mybir as mybir
+from concourse.masks import make_identity
+
+K, T, S, H, V = 1024, 2048, 512, 512, 512
+FLOPS = 2 * K * H * (S + V) + 2 * H * S * V
+
+F32 = mybir.dt.float32
+BF16 = mybir.dt.bfloat16
+I32 = mybir.dt.int32
+U32 = mybir.dt.uint32
+U16 = mybir.dt.uint16
+U8 = mybir.dt.uint8
+FP8X4 = mybir.dt.float8_e4m3fn_x4
+ALU = mybir.AluOpType
+TANH = mybir.ActivationFunctionType.Tanh
+
+P = 128
+PACK = 4
+PASSES = K // (P * PACK)
+HALF = 256
+
+
+def tile_picked_yhnet_grad_p_kernel(
+    tc, x_words, x_scales, w1, unit, inv, sim, wt, offs, other, out
+):
+    nc = tc.nc
+    with ExitStack() as ctx:
+        keep = ctx.enter_context(tc.tile_pool(name="keep", bufs=1))
+        psum = ctx.enter_context(tc.psum_pool(name="psum", bufs=1))
+
+        def sb(name, shape, dtype, tag=None):
+            return keep.tile(shape, dtype, name=name, tag=tag or name, align_bytes=64)
+
+        def bank(name, b):
+            return psum.tile([P, 512], F32, name=name, tag="bank%d" % b)
+
+        list_a = keep.tile([P, S // 16], U16, name="list_a")
+        list_b = keep.tile([P, V // 16], U16, name="list_b")
+        word_table = [sb("word_table%d" % o, [P, T], U32) for o in range(PASSES)]
+        w_raw = [sb("w_raw%d" % o, [P, PACK, H], F32, tag="big%d" % o) for o in range(PASSES)]
+        scale_table = sb("scale_table", [P, T], U8)
+        factor_rows = sb("factor_rows", [P, P], F32)
+        warm = sb("warm", [P, 1], F32)
+
+        def load_words(o):
+            nc.sync.dma_start(
+                word_table[o][:].bitcast(I32),
+                x_words[o].rearrange("p n t -> p (n t)").bitcast(I32),
+            )
+
+        def load_weights(o):
+            nc.sync.dma_start(
+                w_raw[o][:], w1[512 * o : 512 * (o + 1), :].rearrange("(p j) c -> p j c", j=PACK)
+            )
+
+        nc.vector.memset(scale_table[:].bitcast(I32), 0)
+        nc.vector.memset(factor_rows[:], 0.0)
+        nc.scalar.activation(warm[:], factor_rows[:, 0:1], TANH)
+        load_words(0)
+        nc.sync.dma_start(list_b[:], other)
+        nc.sync.dma_start(list_a[:], offs)
+        for q in range(4):
+            nc.sync.dma_start(
+                scale_table[32 * q : 32 * q + 8, :].bitcast(I32),
+                x_scales[:, 4 * q : 4 * q + 4, :].bitcast(I32),
+            )
+        load_weights(0)
+        for r, vec in enumerate((unit, inv)):
+            nc.sync.dma_start(
+                factor_rows[4 * r : 4 * r + 4, :].rearrange("t (g q) -> t g q", q=8),
+                vec.rearrange("(g t q) one -> t g (q one)", t=PACK, q=8),
+            )
+        load_weights(1)
+        load_words(1)
+
+        ident = sb("ident", [P, P], F32)
+        make_identity(nc, ident[:])
+        turned = bank("turned", 7)
+        nc.tensor.transpose(turned[:, 0:P], factor_rows[:], ident[:])
+        factors = sb("factors", [P, 2 * PACK], F32)
+        nc.scalar.copy(factors[:], turned[:, 0 : 2 * PACK])
+
+        lists = {"a": list_a, "b": list_b}
+        x_scale = {}
+        x_code = {}
+        for side in ("b", "a"):
+            x_scale[side] = sb("x_scale_" + side, [P, 512], U8)
+            for o in range(PASSES):
+                x_code[side, o] = sb("x_code_%s%d" % (side, o), [P, 512], U32)
+
+        def gather_words(side, o, c0, width):
+            nc.vector.tensor_copy(
+                x_code[side, o][:, c0 : c0 + width],
+                word_table[o][:].indirect(lists[side][:, c0 // 16 : (c0 + width) // 16]),
+            )
+
+        def gather_scales(side):
+            nc.vector.tensor_copy(x_scale[side][:], scale_table[:].indirect(lists[side][:]))
+
+        w_code = {}
+        w_scale = {}
+        w_bf = {}
+
+        for o in range(PASSES):
+            for u in range(2):
+                w_bf[o, u] = sb("w_bf%d%d" % (o, u), [P, 2, P * PACK], BF16)
+                w_code[o, u] = sb("w_code%d%d" % (o, u), [P, 2 * P], U32)
+                w_scale[o, u] = sb("w_scale%d%d" % (o, u), [P, 2 * P], U8)
+
+        def cast_w(o, t, on_vector):
+            src = w_raw[o][:].rearrange("p j (g t r e) -> p t g r j e", t=PACK, r=4, e=2)[:, t]
+            dst = w_bf[o, t // 2][:, t % 2, :].rearrange("p (g r e j) -> p g r j e", r=4, e=2, j=PACK)
+            if on_vector:
+                nc.vector.tensor_copy(dst, src)
+            else:
+                nc.scalar.copy(dst, src)
+
+        def quant_w(o, u):
+            nc.vector.quantize_mx(
+                out=w_code[o, u][:].bitcast(FP8X4),
+                scales=w_scale[o, u][:],
+                in_=w_bf[o, u][:].rearrange("p t n -> p (t n)"),
+            )
+
+        z = {}
+        for s, side in enumerate(("b", "a")):
+            for h in range(2):
+                for u in range(2):
+                    z[side, h, u] = bank("z_%s%d%d" % (side, h, u), 4 * s + 2 * h + u)
+
+        def first_product(o, side, h, t):
+            cols = slice(HALF * h, HALF * (h + 1))
+            nc.tensor.matmul_mx(
+                out=z[side, h, t // 2][:, HALF * (t % 2) : HALF * (t % 2 + 1)],
+                lhsT=w_code[o, t // 2][:, P * (t % 2) : P * (t % 2 + 1)].bitcast(FP8X4),
+                lhsT_scale=w_scale[o, t // 2][:, P * (t % 2) : P * (t % 2 + 1)],
+                rhs=x_code[side, o][:, cols].bitcast(FP8X4),
+                rhs_scale=x_scale[side][4 * o : P, cols],
+                start=(o == 0),
+                stop=(o == PASSES - 1),
+            )
+
+        for side in ("b", "a"):
+            gather_words(side, 0, 0, 512)
+        for side in ("b", "a"):
+            gather_scales(side)
+        for t in range(PACK):
+            cast_w(0, t, False)
+        for u in range(2):
+            quant_w(0, u)
+        for side in ("b", "a"):
+            for h in range(2):
+                for t in (0, 2):
+                    first_product(0, side, h, t)
+        for t in range(PACK):
+            cast_w(1, t, t == 3)
+        for u in range(2):
+            quant_w(1, u)
+        for side in ("b", "a"):
+            for h in range(2):
+                gather_words(side, 1, HALF * h, HALF)
+        for side in ("b", "a"):
+            for h in range(2):
+                for t in (0, 2):
+                    first_product(1, side, h, t)
+                    first_product(0, side, h, t + 1)
+                    first_product(1, side, h, t + 1)
+
+        sim_sb = sb("sim_sb", [P, 4, V], F32, tag="big0")
+        wt_sb = sb("wt_sb", [P, 4, V], F32, tag="big1")
+        nc.sync.dma_start(sim_sb[:], sim.rearrange("(c p) v -> p c v", p=P))
+        nc.sync.dma_start(wt_sb[:], wt.rearrange("(c p) v -> p c v", p=P))
+
+        th = {}
+
+        def tanh_half(side, h):
+            th[side, h] = sb("th_%s%d" % (side, h), [P, PACK, HALF], F32)
+            for u in range(2):
+                nc.scalar.activation(
+                    th[side, h][:, 2 * u : 2 * u + 2, :].rearrange("p t n -> p (t n)"),
+                    z[side, h, u][:],
+                    TANH,
+                    scale=2.0,
+                )
+
+        h_bf = {}
+
+        def scale_h(side, c0, width):
+            h_bf[side, c0] = sb("h_bf_%s%d" % (side, c0), [P, width * PACK], BF16)
+            lo = c0 % HALF
+            f0 = 0 if side == "a" else PACK
+            nc.vector.tensor_tensor(
+                h_bf[side, c0][:].rearrange("p (n e t) -> p n t e", e=2, t=PACK),
+                th[side, c0 // HALF][:, :, lo : lo + width].rearrange("p t (n e) -> p n t e", e=2),
+                factors[:, f0 : f0 + PACK]
+                .rearrange("p (n t e) -> p n t e", n=1, e=1)
+                .to_broadcast([P, width // 2, PACK, 2]),
+                ALU.mult,
+            )
+
+        h_code = {side: sb("h_code_" + side, [P, 512], U32) for side in ("a", "b")}
+        h_scale = {side: sb("h_scale_" + side, [P, 512], U8) for side in ("a", "b")}
+
+        def quant_h(side, c0, width):
+            nc.vector.quantize_mx(
+                out=h_code[side][:, c0 : c0 + width].bitcast(FP8X4),
+                scales=h_scale[side][:, c0 : c0 + width],
+                in_=h_bf[side, c0][:],
+            )
+
+        half_tanh = {}
+
+        def second_product(c):
+            y = bank("y%d" % c, c)
+            nc.tensor.matmul_mx(
+                out=y[:],
+                lhsT=h_code["a"][:, P * c : P * (c + 1)].bitcast(FP8X4),
+                lhsT_scale=h_scale["a"][:, P * c : P * (c + 1)],
+                rhs=h_code["b"][:].bitcast(FP8X4),
+                rhs_scale=h_scale["b"][:],
+                start=True,
+                stop=True,
+            )
+            half_tanh[c] = sb("half_tanh%d" % c, [P, V], F32)
+            nc.scalar.activation(half_tanh[c][:], y[:], TANH, scale=0.5)
+
+        diff = {}
+
+        def finish_first(c, cols):
+            diff[c, cols.start] = sb("diff%d_%d" % (c, cols.start), [P, cols.stop - cols.start], F32)
+            nc.vector.scalar_tensor_tensor(
+                diff[c, cols.start][:], half_tanh[c][:, cols], 0.5, sim_sb[:, c, cols], ALU.mult, ALU.subtract
+            )
+
+        def finish_second(c, cols):
+            res = sb("res%d_%d" % (c, cols.start), [P, cols.stop - cols.start], F32)
+            nc.vector.scalar_tensor_tensor(
+                res[:], diff[c, cols.start][:], 0.5, wt_sb[:, c, cols], ALU.add, ALU.mult
+            )
+            nc.sync.dma_start(out[P * c : P * (c + 1), cols], res[:])
+
+        for side in ("b", "a"):
+            for h in range(2):
+                tanh_half(side, h)
+        scale_h("b", 0, HALF)
+        scale_h("b", HALF, HALF)
+        quant_h("b", 0, HALF)
+        scale_h("a", 0, P)
+        quant_h("b", HALF, HALF)
+        for c in range(4):
+            if c < 3:
+                scale_h("a", P * (c + 1), P)
+            quant_h("a", P * c, P)
+            second_product(c)
+        pieces = [(c, slice(0, V)) for c in range(3)] + [(3, slice(0, HALF)), (3, slice(HALF, V))]
+        finish_first(*pieces[0])
+        for n, piece in enumerate(pieces):
+            if n + 1 < len(pieces):
+                finish_first(*pieces[n + 1])
+            finish_second(*piece)

@@ -15,11 +15,13 @@ U8 = mybir.dt.uint8
 FP8X4 = mybir.dt.float8_e4m3fn_x4
 ALU = mybir.AluOpType
 TANH = mybir.ActivationFunctionType.Tanh
+COPY = mybir.ActivationFunctionType.Copy
 
 P = 128
 PACK = 4
 PASSES = K // (P * PACK)
 HALF = 256
+CHUNKS = 4
 
 
 def tile_picked_yhnet_grad_p_kernel(
@@ -36,13 +38,16 @@ def tile_picked_yhnet_grad_p_kernel(
         def bank(name, b):
             return psum.tile([P, 512], F32, name=name, tag="bank%d" % b)
 
+        def block(c):
+            return slice(P * c, P * (c + 1))
+
         list_a = keep.tile([P, S // 16], U16, name="list_a")
         list_b = keep.tile([P, V // 16], U16, name="list_b")
         word_table = [sb("word_table%d" % o, [P, T], U32) for o in range(PASSES)]
         w_raw = [sb("w_raw%d" % o, [P, PACK, H], F32, tag="big%d" % o) for o in range(PASSES)]
         scale_table = sb("scale_table", [P, T], U8)
-        factor_rows = sb("factor_rows", [P, P], F32)
-        warm = sb("warm", [P, 1], F32)
+        factor = {side: sb("factor_" + side, [P, PACK], F32) for side in ("b", "a")}
+        warm = sb("warm", [P, 2], F32)
 
         def load_words(o):
             nc.sync.dma_start(
@@ -56,8 +61,8 @@ def tile_picked_yhnet_grad_p_kernel(
             )
 
         nc.vector.memset(scale_table[:].bitcast(I32), 0)
-        nc.vector.memset(factor_rows[:], 0.0)
-        nc.scalar.activation(warm[:], factor_rows[:, 0:1], TANH)
+        nc.vector.memset(warm[:, 0:1], 0.0)
+        nc.scalar.activation(warm[:, 1:2], warm[:, 0:1], TANH)
         load_words(0)
         nc.sync.dma_start(list_b[:], other)
         nc.sync.dma_start(list_a[:], offs)
@@ -67,29 +72,15 @@ def tile_picked_yhnet_grad_p_kernel(
                 x_scales[:, 4 * q : 4 * q + 4, :].bitcast(I32),
             )
         load_weights(0)
-        for r, vec in enumerate((unit, inv)):
-            nc.sync.dma_start(
-                factor_rows[4 * r : 4 * r + 4, :].rearrange("t (g q) -> t g q", q=8),
-                vec.rearrange("(g t q) one -> t g (q one)", t=PACK, q=8),
-            )
         load_weights(1)
         load_words(1)
+        nc.sync.dma_start(factor["b"][:], inv.rearrange("(p t) one -> p (t one)", t=PACK))
+        nc.sync.dma_start(factor["a"][:], unit.rearrange("(p t) one -> p (t one)", t=PACK))
 
         ident = sb("ident", [P, P], F32)
         make_identity(nc, ident[:])
-        turned = bank("turned", 7)
-        nc.tensor.transpose(turned[:, 0:P], factor_rows[:], ident[:])
-        factors = sb("factors", [P, 2 * PACK], F32)
-        nc.scalar.copy(factors[:], turned[:, 0 : 2 * PACK])
 
         lists = {"a": list_a, "b": list_b}
-        x_scale = {}
-        x_code = {}
-        for side in ("b", "a"):
-            x_scale[side] = sb("x_scale_" + side, [P, 512], U8)
-            for o in range(PASSES):
-                x_code[side, o] = sb("x_code_%s%d" % (side, o), [P, 512], U32)
-
         def gather_words(side, o, c0, width):
             nc.vector.tensor_copy(
                 x_code[side, o][:, c0 : c0 + width],
@@ -102,16 +93,24 @@ def tile_picked_yhnet_grad_p_kernel(
         w_code = {}
         w_scale = {}
         w_bf = {}
-
         for o in range(PASSES):
             for u in range(2):
                 w_bf[o, u] = sb("w_bf%d%d" % (o, u), [P, 2, P * PACK], BF16)
                 w_code[o, u] = sb("w_code%d%d" % (o, u), [P, 2 * P], U32)
                 w_scale[o, u] = sb("w_scale%d%d" % (o, u), [P, 2 * P], U8)
 
-        def cast_w(o, t, on_vector):
-            src = w_raw[o][:].rearrange("p j (g t r e) -> p t g r j e", t=PACK, r=4, e=2)[:, t]
-            dst = w_bf[o, t // 2][:, t % 2, :].rearrange("p (g r e j) -> p g r j e", r=4, e=2, j=PACK)
+        x_scale = {
+            "b": sb("x_scale_b", [P, 512], U8),
+            "a": sb("x_scale_a", [P, 512], U8),
+        }
+        x_code = {}
+        for side in ("b", "a"):
+            for o in range(PASSES):
+                x_code[side, o] = sb("x_code_%s%d" % (side, o), [P, 512], U32)
+
+        def cast_w(o, u, on_vector):
+            src = w_raw[o][:].rearrange("p j (m u e) -> p u m j e", u=2, e=2)[:, u]
+            dst = w_bf[o, u][:].rearrange("p e (m j) -> p m j e", j=PACK)
             if on_vector:
                 nc.vector.tensor_copy(dst, src)
             else:
@@ -126,88 +125,72 @@ def tile_picked_yhnet_grad_p_kernel(
 
         z = {}
         for s, side in enumerate(("b", "a")):
-            for h in range(2):
-                for u in range(2):
-                    z[side, h, u] = bank("z_%s%d%d" % (side, h, u), 4 * s + 2 * h + u)
+            for c in range(CHUNKS):
+                z[side, c] = bank("z_%s%d" % (side, c), CHUNKS * s + c)
 
-        def first_product(o, side, h, t):
-            cols = slice(HALF * h, HALF * (h + 1))
-            nc.tensor.matmul_mx(
-                out=z[side, h, t // 2][:, HALF * (t % 2) : HALF * (t % 2 + 1)],
-                lhsT=w_code[o, t // 2][:, P * (t % 2) : P * (t % 2 + 1)].bitcast(FP8X4),
-                lhsT_scale=w_scale[o, t // 2][:, P * (t % 2) : P * (t % 2 + 1)],
-                rhs=x_code[side, o][:, cols].bitcast(FP8X4),
-                rhs_scale=x_scale[side][4 * o : P, cols],
-                start=(o == 0),
-                stop=(o == PASSES - 1),
-            )
+        def first_product(o, side, c, first):
+            for t in range(PACK):
+                nc.tensor.matmul_mx(
+                    out=z[side, c][:, block(t)],
+                    lhsT=w_code[o, t // 2][:, block(t % 2)].bitcast(FP8X4),
+                    lhsT_scale=w_scale[o, t // 2][:, block(t % 2)],
+                    rhs=x_code[side, o][:, block(c)].bitcast(FP8X4),
+                    rhs_scale=x_scale[side][4 * o : P, block(c)],
+                    start=(first and t == 0),
+                    stop=(not first and t == PACK - 1),
+                )
 
         for side in ("b", "a"):
             gather_words(side, 0, 0, 512)
         for side in ("b", "a"):
             gather_scales(side)
-        for t in range(PACK):
-            cast_w(0, t, False)
+        for u in range(2):
+            cast_w(0, u, False)
         for u in range(2):
             quant_w(0, u)
-        for side in ("b", "a"):
-            for h in range(2):
-                for t in (0, 2):
-                    first_product(0, side, h, t)
-        for t in range(PACK):
-            cast_w(1, t, t == 3)
+        for c in range(CHUNKS):
+            first_product(0, "b", c, True)
+        for u in range(2):
+            cast_w(1, u, u == 1)
         for u in range(2):
             quant_w(1, u)
         for side in ("b", "a"):
             for h in range(2):
                 gather_words(side, 1, HALF * h, HALF)
-        for side in ("b", "a"):
-            for h in range(2):
-                for t in (0, 2):
-                    first_product(1, side, h, t)
-                    first_product(0, side, h, t + 1)
-                    first_product(1, side, h, t + 1)
+        for c in range(CHUNKS):
+            first_product(1, "b", c, False)
+        for c in range(CHUNKS):
+            first_product(1, "a", c, True)
+            first_product(0, "a", c, False)
 
-        sim_sb = sb("sim_sb", [P, 4, V], F32, tag="big0")
-        wt_sb = sb("wt_sb", [P, 4, V], F32, tag="big1")
+        sim_sb = sb("sim_sb", [P, CHUNKS, V], F32, tag="big0")
+        wt_sb = sb("wt_sb", [P, CHUNKS, V], F32, tag="big1")
         nc.sync.dma_start(sim_sb[:], sim.rearrange("(c p) v -> p c v", p=P))
         nc.sync.dma_start(wt_sb[:], wt.rearrange("(c p) v -> p c v", p=P))
 
-        th = {}
-
-        def tanh_half(side, h):
-            th[side, h] = sb("th_%s%d" % (side, h), [P, PACK, HALF], F32)
-            for u in range(2):
-                nc.scalar.activation(
-                    th[side, h][:, 2 * u : 2 * u + 2, :].rearrange("p t n -> p (t n)"),
-                    z[side, h, u][:],
-                    TANH,
-                    scale=2.0,
-                )
-
-        h_bf = {}
-
-        def scale_h(side, c0, width):
-            h_bf[side, c0] = sb("h_bf_%s%d" % (side, c0), [P, width * PACK], BF16)
-            lo = c0 % HALF
-            f0 = 0 if side == "a" else PACK
-            nc.vector.tensor_tensor(
-                h_bf[side, c0][:].rearrange("p (n e t) -> p n t e", e=2, t=PACK),
-                th[side, c0 // HALF][:, :, lo : lo + width].rearrange("p t (n e) -> p n t e", e=2),
-                factors[:, f0 : f0 + PACK]
-                .rearrange("p (n t e) -> p n t e", n=1, e=1)
-                .to_broadcast([P, width // 2, PACK, 2]),
-                ALU.mult,
-            )
-
+        th = {side: sb("th_" + side, [P, 512, PACK], F32) for side in ("a", "b")}
+        h_bf = {side: sb("h_bf_" + side, [P, 512, PACK], BF16) for side in ("a", "b")}
         h_code = {side: sb("h_code_" + side, [P, 512], U32) for side in ("a", "b")}
         h_scale = {side: sb("h_scale_" + side, [P, 512], U8) for side in ("a", "b")}
+
+        def steep_tanh(side, c):
+            nc.scalar.activation(
+                th[side][:, block(c), :], z[side, c][:].rearrange("p (t n) -> p n t", t=PACK), TANH, scale=2.0
+            )
+
+        def scale_h(side, c0, width):
+            nc.vector.tensor_tensor(
+                h_bf[side][:, c0 : c0 + width, :],
+                th[side][:, c0 : c0 + width, :],
+                factor[side][:].rearrange("p (n t) -> p n t", n=1).to_broadcast([P, width, PACK]),
+                ALU.mult,
+            )
 
         def quant_h(side, c0, width):
             nc.vector.quantize_mx(
                 out=h_code[side][:, c0 : c0 + width].bitcast(FP8X4),
                 scales=h_scale[side][:, c0 : c0 + width],
-                in_=h_bf[side, c0][:],
+                in_=h_bf[side][:, c0 : c0 + width, :].rearrange("p n t -> p (n t)"),
             )
 
         half_tanh = {}
@@ -216,8 +199,8 @@ def tile_picked_yhnet_grad_p_kernel(
             y = bank("y%d" % c, c)
             nc.tensor.matmul_mx(
                 out=y[:],
-                lhsT=h_code["a"][:, P * c : P * (c + 1)].bitcast(FP8X4),
-                lhsT_scale=h_scale["a"][:, P * c : P * (c + 1)],
+                lhsT=h_code["a"][:, block(c)].bitcast(FP8X4),
+                lhsT_scale=h_scale["a"][:, block(c)],
                 rhs=h_code["b"][:].bitcast(FP8X4),
                 rhs_scale=h_scale["b"][:],
                 start=True,
@@ -225,6 +208,49 @@ def tile_picked_yhnet_grad_p_kernel(
             )
             half_tanh[c] = sb("half_tanh%d" % c, [P, V], F32)
             nc.scalar.activation(half_tanh[c][:], y[:], TANH, scale=0.5)
+
+        total = {}
+
+        def open_total(c):
+            sim_turned = bank("sim_turned%d" % c, c)
+            for d in range(CHUNKS):
+                nc.tensor.transpose(sim_turned[:, block(d)], sim_sb[:, c, block(d)], ident[:])
+            sign = sb("sign%d" % c, [P, V], F32)
+            nc.scalar.activation(sign[:], sim_turned[:], COPY, bias=1.0, scale=-2.0)
+            total[c] = bank("total%d" % c, c)
+            for d in range(CHUNKS):
+                nc.tensor.matmul(
+                    total[c][:, block(d)], sign[:, block(d)], ident[:], start=(d == 0), stop=False, is_transpose=True
+                )
+
+        def turned_product(c):
+            y = bank("y%d" % c, CHUNKS + c)
+            for d in range(CHUNKS):
+                nc.tensor.matmul_mx(
+                    out=y[:, block(d)],
+                    lhsT=h_code["b"][:, block(d)].bitcast(FP8X4),
+                    lhsT_scale=h_scale["b"][:, block(d)],
+                    rhs=h_code["a"][:, block(c)].bitcast(FP8X4),
+                    rhs_scale=h_scale["a"][:, block(c)],
+                    start=True,
+                    stop=True,
+                )
+            half_tanh[c] = sb("half_tanh%d" % c, [P, V], F32)
+            nc.scalar.activation(half_tanh[c][:], y[:], TANH, scale=0.5)
+            for d in range(CHUNKS):
+                nc.tensor.matmul(
+                    total[c][:, block(d)],
+                    half_tanh[c][:, block(d)],
+                    ident[:],
+                    start=False,
+                    stop=(d == CHUNKS - 1),
+                    is_transpose=True,
+                )
+
+        def finish_total(c, cols):
+            res = sb("res%d_%d" % (c, cols.start), [P, cols.stop - cols.start], F32)
+            nc.vector.scalar_tensor_tensor(res[:], total[c][:, cols], 0.5, wt_sb[:, c, cols], ALU.mult, ALU.mult)
+            nc.sync.dma_start(out[block(c), cols], res[:])
 
         diff = {}
 
@@ -239,24 +265,31 @@ def tile_picked_yhnet_grad_p_kernel(
             nc.vector.scalar_tensor_tensor(
                 res[:], diff[c, cols.start][:], 0.5, wt_sb[:, c, cols], ALU.add, ALU.mult
             )
-            nc.sync.dma_start(out[P * c : P * (c + 1), cols], res[:])
+            nc.sync.dma_start(out[block(c), cols], res[:])
 
         for side in ("b", "a"):
-            for h in range(2):
-                tanh_half(side, h)
+            for c in range(CHUNKS):
+                steep_tanh(side, c)
+        for c in range(2, CHUNKS):
+            open_total(c)
         scale_h("b", 0, HALF)
         scale_h("b", HALF, HALF)
         quant_h("b", 0, HALF)
         scale_h("a", 0, P)
         quant_h("b", HALF, HALF)
-        for c in range(4):
-            if c < 3:
+        for c in range(CHUNKS):
+            if c + 1 < CHUNKS:
                 scale_h("a", P * (c + 1), P)
             quant_h("a", P * c, P)
-            second_product(c)
-        pieces = [(c, slice(0, V)) for c in range(3)] + [(3, slice(0, HALF)), (3, slice(HALF, V))]
-        finish_first(*pieces[0])
-        for n, piece in enumerate(pieces):
-            if n + 1 < len(pieces):
-                finish_first(*pieces[n + 1])
-            finish_second(*piece)
+            if c < 2:
+                second_product(c)
+            else:
+                turned_product(c)
+        for c in range(2):
+            finish_first(c, slice(0, V))
+        for c in range(2):
+            finish_second(c, slice(0, V))
+        for c in range(2, CHUNKS - 1):
+            finish_total(c, slice(0, V))
+        finish_total(CHUNKS - 1, slice(0, HALF))
+        finish_total(CHUNKS - 1, slice(HALF, V))

@@ -19,9 +19,15 @@ COPY = mybir.ActivationFunctionType.Copy
 
 P = 128
 PACK = 4
-PASSES = K // (P * PACK)
-HALF = 256
-CHUNKS = 4
+K_PASS = P * PACK
+PASSES = K // K_PASS
+ENTRIES = S
+HALF = ENTRIES // 2
+CHUNKS = ENTRIES // P
+BANK = 512
+QUADRANT = 32
+SCALE_ROWS = 4
+FIRST_TURNED = 2
 
 
 def tile_picked_yhnet_grad_p_kernel(
@@ -35,11 +41,11 @@ def tile_picked_yhnet_grad_p_kernel(
         def sb(name, shape, dtype, tag=None):
             return keep.tile(shape, dtype, name=name, tag=tag or name, align_bytes=64)
 
-        def bank(name, b):
-            return psum.tile([P, 512], F32, name=name, tag="bank%d" % b)
+        def bank(name, number):
+            return psum.tile([P, BANK], F32, name=name, tag="bank%d" % number)
 
-        def block(c):
-            return slice(P * c, P * (c + 1))
+        def block(n):
+            return slice(P * n, P * (n + 1))
 
         list_a = keep.tile([P, S // 16], U16, name="list_a")
         list_b = keep.tile([P, V // 16], U16, name="list_b")
@@ -47,44 +53,41 @@ def tile_picked_yhnet_grad_p_kernel(
         w_raw = [sb("w_raw%d" % o, [P, PACK, H], F32, tag="big%d" % o) for o in range(PASSES)]
         scale_table = sb("scale_table", [P, T], U8)
         factor = {side: sb("factor_" + side, [P, PACK], F32) for side in ("b", "a")}
-        warm = sb("warm", [P, 2], F32)
 
         def load_words(o):
             nc.sync.dma_start(
                 word_table[o][:].bitcast(I32),
-                x_words[o].rearrange("p n t -> p (n t)").bitcast(I32),
+                x_words[o].rearrange("p n j -> p (n j)").bitcast(I32),
             )
 
         def load_weights(o):
-            nc.sync.dma_start(
-                w_raw[o][:], w1[512 * o : 512 * (o + 1), :].rearrange("(p j) c -> p j c", j=PACK)
-            )
+            rows = w1[K_PASS * o : K_PASS * (o + 1), :]
+            nc.sync.dma_start(w_raw[o][:], rows.rearrange("(p j) c -> p j c", j=PACK))
 
         nc.vector.memset(scale_table[:].bitcast(I32), 0)
-        nc.vector.memset(warm[:, 0:1], 0.0)
-        nc.scalar.activation(warm[:, 1:2], warm[:, 0:1], TANH)
         load_words(0)
         nc.sync.dma_start(list_b[:], other)
         nc.sync.dma_start(list_a[:], offs)
-        for q in range(4):
+        for q in range(P // QUADRANT):
             nc.sync.dma_start(
-                scale_table[32 * q : 32 * q + 8, :].bitcast(I32),
-                x_scales[:, 4 * q : 4 * q + 4, :].bitcast(I32),
+                scale_table[QUADRANT * q : QUADRANT * q + PASSES * SCALE_ROWS, :].bitcast(I32),
+                x_scales[:, SCALE_ROWS * q : SCALE_ROWS * (q + 1), :].bitcast(I32),
             )
         load_weights(0)
         load_weights(1)
         load_words(1)
-        nc.sync.dma_start(factor["b"][:], inv.rearrange("(p t) one -> p (t one)", t=PACK))
-        nc.sync.dma_start(factor["a"][:], unit.rearrange("(p t) one -> p (t one)", t=PACK))
+        nc.sync.dma_start(factor["b"][:], inv.rearrange("(p s) one -> p (s one)", s=PACK))
+        nc.sync.dma_start(factor["a"][:], unit.rearrange("(p s) one -> p (s one)", s=PACK))
 
         ident = sb("ident", [P, P], F32)
         make_identity(nc, ident[:])
 
         lists = {"a": list_a, "b": list_b}
-        def gather_words(side, o, c0, width):
+
+        def gather_words(side, o, first_entry, count):
             nc.vector.tensor_copy(
-                x_code[side, o][:, c0 : c0 + width],
-                word_table[o][:].indirect(lists[side][:, c0 // 16 : (c0 + width) // 16]),
+                x_code[side, o][:, first_entry : first_entry + count],
+                word_table[o][:].indirect(lists[side][:, first_entry // 16 : (first_entry + count) // 16]),
             )
 
         def gather_scales(side):
@@ -94,66 +97,63 @@ def tile_picked_yhnet_grad_p_kernel(
         w_scale = {}
         w_bf = {}
         for o in range(PASSES):
-            for u in range(2):
-                w_bf[o, u] = sb("w_bf%d%d" % (o, u), [P, 2, P * PACK], BF16)
-                w_code[o, u] = sb("w_code%d%d" % (o, u), [P, 2 * P], U32)
-                w_scale[o, u] = sb("w_scale%d%d" % (o, u), [P, 2 * P], U8)
+            for pair in range(2):
+                w_bf[o, pair] = sb("w_bf%d%d" % (o, pair), [P, 2, P * PACK], BF16)
+                w_code[o, pair] = sb("w_code%d%d" % (o, pair), [P, 2 * P], U32)
+                w_scale[o, pair] = sb("w_scale%d%d" % (o, pair), [P, 2 * P], U8)
 
-        x_scale = {
-            "b": sb("x_scale_b", [P, 512], U8),
-            "a": sb("x_scale_a", [P, 512], U8),
-        }
+        x_scale = {side: sb("x_scale_" + side, [P, ENTRIES], U8) for side in ("b", "a")}
         x_code = {}
         for side in ("b", "a"):
             for o in range(PASSES):
-                x_code[side, o] = sb("x_code_%s%d" % (side, o), [P, 512], U32)
+                x_code[side, o] = sb("x_code_%s%d" % (side, o), [P, ENTRIES], U32)
 
-        def cast_w(o, u, on_vector):
-            src = w_raw[o][:].rearrange("p j (m u e) -> p u m j e", u=2, e=2)[:, u]
-            dst = w_bf[o, u][:].rearrange("p e (m j) -> p m j e", j=PACK)
+        def cast_w(o, pair, on_vector):
+            src = w_raw[o][:].rearrange("p j (m pair e) -> p pair m j e", pair=2, e=2)[:, pair]
+            dst = w_bf[o, pair][:].rearrange("p e (m j) -> p m j e", j=PACK)
             if on_vector:
                 nc.vector.tensor_copy(dst, src)
             else:
                 nc.scalar.copy(dst, src)
 
-        def quant_w(o, u):
+        def quant_w(o, pair):
             nc.vector.quantize_mx(
-                out=w_code[o, u][:].bitcast(FP8X4),
-                scales=w_scale[o, u][:],
-                in_=w_bf[o, u][:].rearrange("p t n -> p (t n)"),
+                out=w_code[o, pair][:].bitcast(FP8X4),
+                scales=w_scale[o, pair][:],
+                in_=w_bf[o, pair][:].rearrange("p e n -> p (e n)"),
             )
 
         z = {}
-        for s, side in enumerate(("b", "a")):
+        for n, side in enumerate(("b", "a")):
             for c in range(CHUNKS):
-                z[side, c] = bank("z_%s%d" % (side, c), CHUNKS * s + c)
+                z[side, c] = bank("z_%s%d" % (side, c), CHUNKS * n + c)
 
-        def first_product(o, side, c, first):
-            for t in range(PACK):
+        def first_product(o, side, c, opens):
+            for s in range(PACK):
                 nc.tensor.matmul_mx(
-                    out=z[side, c][:, block(t)],
-                    lhsT=w_code[o, t // 2][:, block(t % 2)].bitcast(FP8X4),
-                    lhsT_scale=w_scale[o, t // 2][:, block(t % 2)],
+                    out=z[side, c][:, block(s)],
+                    lhsT=w_code[o, s // 2][:, block(s % 2)].bitcast(FP8X4),
+                    lhsT_scale=w_scale[o, s // 2][:, block(s % 2)],
                     rhs=x_code[side, o][:, block(c)].bitcast(FP8X4),
-                    rhs_scale=x_scale[side][4 * o : P, block(c)],
-                    start=(first and t == 0),
-                    stop=(not first and t == PACK - 1),
+                    rhs_scale=x_scale[side][SCALE_ROWS * o : P, block(c)],
+                    start=(opens and s == 0),
+                    stop=(not opens and s == PACK - 1),
                 )
 
         for side in ("b", "a"):
-            gather_words(side, 0, 0, 512)
+            gather_words(side, 0, 0, ENTRIES)
         for side in ("b", "a"):
             gather_scales(side)
-        for u in range(2):
-            cast_w(0, u, False)
-        for u in range(2):
-            quant_w(0, u)
+        for pair in range(2):
+            cast_w(0, pair, False)
+        for pair in range(2):
+            quant_w(0, pair)
         for c in range(CHUNKS):
             first_product(0, "b", c, True)
-        for u in range(2):
-            cast_w(1, u, u == 1)
-        for u in range(2):
-            quant_w(1, u)
+        for pair in range(2):
+            cast_w(1, pair, pair == 1)
+        for pair in range(2):
+            quant_w(1, pair)
         for side in ("b", "a"):
             for h in range(2):
                 gather_words(side, 1, HALF * h, HALF)
@@ -168,32 +168,37 @@ def tile_picked_yhnet_grad_p_kernel(
         nc.sync.dma_start(sim_sb[:], sim.rearrange("(c p) v -> p c v", p=P))
         nc.sync.dma_start(wt_sb[:], wt.rearrange("(c p) v -> p c v", p=P))
 
-        th = {side: sb("th_" + side, [P, 512, PACK], F32) for side in ("a", "b")}
-        h_bf = {side: sb("h_bf_" + side, [P, 512, PACK], BF16) for side in ("a", "b")}
-        h_code = {side: sb("h_code_" + side, [P, 512], U32) for side in ("a", "b")}
-        h_scale = {side: sb("h_scale_" + side, [P, 512], U8) for side in ("a", "b")}
+        th = {side: sb("th_" + side, [P, ENTRIES, PACK], F32) for side in ("a", "b")}
+        h_bf = {side: sb("h_bf_" + side, [P, ENTRIES, PACK], BF16) for side in ("a", "b")}
+        h_code = {side: sb("h_code_" + side, [P, ENTRIES], U32) for side in ("a", "b")}
+        h_scale = {side: sb("h_scale_" + side, [P, ENTRIES], U8) for side in ("a", "b")}
 
         def steep_tanh(side, c):
             nc.scalar.activation(
-                th[side][:, block(c), :], z[side, c][:].rearrange("p (t n) -> p n t", t=PACK), TANH, scale=2.0
+                th[side][:, block(c), :],
+                z[side, c][:].rearrange("p (s n) -> p n s", s=PACK),
+                TANH,
+                scale=2.0,
             )
 
-        def scale_h(side, c0, width):
+        def scale_h(side, first_entry, count):
             nc.vector.tensor_tensor(
-                h_bf[side][:, c0 : c0 + width, :],
-                th[side][:, c0 : c0 + width, :],
-                factor[side][:].rearrange("p (n t) -> p n t", n=1).to_broadcast([P, width, PACK]),
+                h_bf[side][:, first_entry : first_entry + count, :],
+                th[side][:, first_entry : first_entry + count, :],
+                factor[side][:].rearrange("p (n s) -> p n s", n=1).to_broadcast([P, count, PACK]),
                 ALU.mult,
             )
 
-        def quant_h(side, c0, width):
+        def quant_h(side, first_entry, count):
             nc.vector.quantize_mx(
-                out=h_code[side][:, c0 : c0 + width].bitcast(FP8X4),
-                scales=h_scale[side][:, c0 : c0 + width],
-                in_=h_bf[side][:, c0 : c0 + width, :].rearrange("p n t -> p (n t)"),
+                out=h_code[side][:, first_entry : first_entry + count].bitcast(FP8X4),
+                scales=h_scale[side][:, first_entry : first_entry + count],
+                in_=h_bf[side][:, first_entry : first_entry + count, :].rearrange("p n s -> p (n s)"),
             )
 
         half_tanh = {}
+        diff = {}
+        total = {}
 
         def second_product(c):
             y = bank("y%d" % c, c)
@@ -209,18 +214,21 @@ def tile_picked_yhnet_grad_p_kernel(
             half_tanh[c] = sb("half_tanh%d" % c, [P, V], F32)
             nc.scalar.activation(half_tanh[c][:], y[:], TANH, scale=0.5)
 
-        total = {}
-
         def open_total(c):
             sim_turned = bank("sim_turned%d" % c, c)
             for d in range(CHUNKS):
                 nc.tensor.transpose(sim_turned[:, block(d)], sim_sb[:, c, block(d)], ident[:])
-            sign = sb("sign%d" % c, [P, V], F32)
-            nc.scalar.activation(sign[:], sim_turned[:], COPY, bias=1.0, scale=-2.0)
+            sim_term = sb("sim_term%d" % c, [P, V], F32)
+            nc.scalar.activation(sim_term[:], sim_turned[:], COPY, bias=1.0, scale=-2.0)
             total[c] = bank("total%d" % c, c)
             for d in range(CHUNKS):
                 nc.tensor.matmul(
-                    total[c][:, block(d)], sign[:, block(d)], ident[:], start=(d == 0), stop=False, is_transpose=True
+                    total[c][:, block(d)],
+                    sim_term[:, block(d)],
+                    ident[:],
+                    start=(d == 0),
+                    stop=False,
+                    is_transpose=True,
                 )
 
         def turned_product(c):
@@ -252,25 +260,19 @@ def tile_picked_yhnet_grad_p_kernel(
             nc.vector.scalar_tensor_tensor(res[:], total[c][:, cols], 0.5, wt_sb[:, c, cols], ALU.mult, ALU.mult)
             nc.sync.dma_start(out[block(c), cols], res[:])
 
-        diff = {}
+        def subtract_sim(c):
+            diff[c] = sb("diff%d" % c, [P, V], F32)
+            nc.vector.scalar_tensor_tensor(diff[c][:], half_tanh[c][:], 0.5, sim_sb[:, c, :], ALU.mult, ALU.subtract)
 
-        def finish_first(c, cols):
-            diff[c, cols.start] = sb("diff%d_%d" % (c, cols.start), [P, cols.stop - cols.start], F32)
-            nc.vector.scalar_tensor_tensor(
-                diff[c, cols.start][:], half_tanh[c][:, cols], 0.5, sim_sb[:, c, cols], ALU.mult, ALU.subtract
-            )
-
-        def finish_second(c, cols):
-            res = sb("res%d_%d" % (c, cols.start), [P, cols.stop - cols.start], F32)
-            nc.vector.scalar_tensor_tensor(
-                res[:], diff[c, cols.start][:], 0.5, wt_sb[:, c, cols], ALU.add, ALU.mult
-            )
-            nc.sync.dma_start(out[block(c), cols], res[:])
+        def finish_diff(c):
+            res = sb("res%d_0" % c, [P, V], F32)
+            nc.vector.scalar_tensor_tensor(res[:], diff[c][:], 0.5, wt_sb[:, c, :], ALU.add, ALU.mult)
+            nc.sync.dma_start(out[block(c), :], res[:])
 
         for side in ("b", "a"):
             for c in range(CHUNKS):
                 steep_tanh(side, c)
-        for c in range(2, CHUNKS):
+        for c in range(FIRST_TURNED, CHUNKS):
             open_total(c)
         scale_h("b", 0, HALF)
         scale_h("b", HALF, HALF)
@@ -281,15 +283,15 @@ def tile_picked_yhnet_grad_p_kernel(
             if c + 1 < CHUNKS:
                 scale_h("a", P * (c + 1), P)
             quant_h("a", P * c, P)
-            if c < 2:
+            if c < FIRST_TURNED:
                 second_product(c)
             else:
                 turned_product(c)
-        for c in range(2):
-            finish_first(c, slice(0, V))
-        for c in range(2):
-            finish_second(c, slice(0, V))
-        for c in range(2, CHUNKS - 1):
+        for c in range(FIRST_TURNED):
+            subtract_sim(c)
+        for c in range(FIRST_TURNED):
+            finish_diff(c)
+        for c in range(FIRST_TURNED, CHUNKS - 1):
             finish_total(c, slice(0, V))
         finish_total(CHUNKS - 1, slice(0, HALF))
         finish_total(CHUNKS - 1, slice(HALF, V))

@@ -27,7 +27,7 @@ CHUNKS = ENTRIES // P
 BANK = 512
 QUADRANT = 32
 SCALE_ROWS = 4
-FIRST_TURNED = 2
+FIRST_TURNED = 1
 
 
 def tile_picked_yhnet_grad_p_kernel(
@@ -154,9 +154,9 @@ def tile_picked_yhnet_grad_p_kernel(
             cast_w(1, pair, pair == 1)
         for pair in range(2):
             quant_w(1, pair)
-        for side in ("b", "a"):
-            for h in range(2):
-                gather_words(side, 1, HALF * h, HALF)
+        for h in range(2):
+            gather_words("b", 1, HALF * h, HALF)
+        gather_words("a", 1, 0, ENTRIES)
         for c in range(CHUNKS):
             first_product(1, "b", c, False)
         for c in range(CHUNKS):
@@ -214,22 +214,28 @@ def tile_picked_yhnet_grad_p_kernel(
             half_tanh[c] = sb("half_tanh%d" % c, [P, V], F32)
             nc.scalar.activation(half_tanh[c][:], y[:], TANH, scale=0.5)
 
+        def pieces(c):
+            if c == CHUNKS - 1:
+                return [(0, 1), (2, 3)]
+            return [(0, 1, 2, 3)]
+
         def open_total(c):
             sim_turned = bank("sim_turned%d" % c, c)
             for d in range(CHUNKS):
                 nc.tensor.transpose(sim_turned[:, block(d)], sim_sb[:, c, block(d)], ident[:])
             sim_term = sb("sim_term%d" % c, [P, V], F32)
             nc.scalar.activation(sim_term[:], sim_turned[:], COPY, bias=1.0, scale=-2.0)
-            total[c] = bank("total%d" % c, c)
-            for d in range(CHUNKS):
-                nc.tensor.matmul(
-                    total[c][:, block(d)],
-                    sim_term[:, block(d)],
-                    ident[:],
-                    start=(d == 0),
-                    stop=False,
-                    is_transpose=True,
-                )
+            for n, piece in enumerate(pieces(c)):
+                total[c, n] = bank("total%d_%d" % (c, n), c + n)
+                for d in piece:
+                    nc.tensor.matmul(
+                        total[c, n][:, block(d)],
+                        sim_term[:, block(d)],
+                        ident[:],
+                        start=(d == piece[0]),
+                        stop=False,
+                        is_transpose=True,
+                    )
 
         def turned_product(c):
             y = bank("y%d" % c, CHUNKS + c)
@@ -244,21 +250,27 @@ def tile_picked_yhnet_grad_p_kernel(
                     stop=True,
                 )
             half_tanh[c] = sb("half_tanh%d" % c, [P, V], F32)
-            nc.scalar.activation(half_tanh[c][:], y[:], TANH, scale=0.5)
-            for d in range(CHUNKS):
-                nc.tensor.matmul(
-                    total[c][:, block(d)],
-                    half_tanh[c][:, block(d)],
-                    ident[:],
-                    start=False,
-                    stop=(d == CHUNKS - 1),
-                    is_transpose=True,
-                )
+            for n, piece in enumerate(pieces(c)):
+                cols = slice(P * piece[0], P * (piece[-1] + 1))
+                nc.scalar.activation(half_tanh[c][:, cols], y[:, cols], TANH, scale=0.5)
+                for d in piece:
+                    nc.tensor.matmul(
+                        total[c, n][:, block(d)],
+                        half_tanh[c][:, block(d)],
+                        ident[:],
+                        start=False,
+                        stop=(d == piece[-1]),
+                        is_transpose=True,
+                    )
 
-        def finish_total(c, cols):
-            res = sb("res%d_%d" % (c, cols.start), [P, cols.stop - cols.start], F32)
-            nc.vector.scalar_tensor_tensor(res[:], total[c][:, cols], 0.5, wt_sb[:, c, cols], ALU.mult, ALU.mult)
-            nc.sync.dma_start(out[block(c), cols], res[:])
+        def finish_total(c):
+            for n, piece in enumerate(pieces(c)):
+                cols = slice(P * piece[0], P * (piece[-1] + 1))
+                res = sb("res%d_%d" % (c, n), [P, cols.stop - cols.start], F32)
+                nc.vector.scalar_tensor_tensor(
+                    res[:], total[c, n][:, cols], 0.5, wt_sb[:, c, cols], ALU.mult, ALU.mult
+                )
+                nc.sync.dma_start(out[block(c), cols], res[:])
 
         def subtract_sim(c):
             diff[c] = sb("diff%d" % c, [P, V], F32)
@@ -291,7 +303,5 @@ def tile_picked_yhnet_grad_p_kernel(
             subtract_sim(c)
         for c in range(FIRST_TURNED):
             finish_diff(c)
-        for c in range(FIRST_TURNED, CHUNKS - 1):
-            finish_total(c, slice(0, V))
-        finish_total(CHUNKS - 1, slice(0, HALF))
-        finish_total(CHUNKS - 1, slice(HALF, V))
+        for c in range(FIRST_TURNED, CHUNKS):
+            finish_total(c)

@@ -64,16 +64,21 @@ def tile_picked_yhnet_grad_p_kernel(
             rows = w1[K_PASS * o : K_PASS * (o + 1), :]
             nc.sync.dma_start(w_raw[o][:], rows.rearrange("(p j) c -> p j c", j=PACK))
 
-        nc.vector.memset(scale_table[:].bitcast(I32), 0)
+        def load_scales(o):
+            for q in range(P // QUADRANT):
+                first = QUADRANT * q + SCALE_ROWS * o
+                nc.sync.dma_start(
+                    scale_table[first : first + SCALE_ROWS, :].bitcast(I32),
+                    x_scales[o, SCALE_ROWS * q : SCALE_ROWS * (q + 1), :].bitcast(I32),
+                )
+
+        nc.gpsimd.memset(scale_table[:].bitcast(I32), 0)
+        load_scales(0)
         load_words(0)
         nc.sync.dma_start(list_b[:], other)
         nc.sync.dma_start(list_a[:], offs)
-        for q in range(P // QUADRANT):
-            nc.sync.dma_start(
-                scale_table[QUADRANT * q : QUADRANT * q + PASSES * SCALE_ROWS, :].bitcast(I32),
-                x_scales[:, SCALE_ROWS * q : SCALE_ROWS * (q + 1), :].bitcast(I32),
-            )
         load_weights(0)
+        load_scales(1)
         load_weights(1)
         load_words(1)
         nc.sync.dma_start(factor["b"][:], inv.rearrange("(p s) one -> p (s one)", s=PACK))
@@ -102,7 +107,7 @@ def tile_picked_yhnet_grad_p_kernel(
                 w_code[o, pair] = sb("w_code%d%d" % (o, pair), [P, 2 * P], U32)
                 w_scale[o, pair] = sb("w_scale%d%d" % (o, pair), [P, 2 * P], U8)
 
-        x_scale = {side: sb("x_scale_" + side, [P, ENTRIES], U8) for side in ("b", "a")}
+        x_scale = {"b": sb("x_scale_b", [P, ENTRIES], U8)}
         x_code = {}
         for side in ("b", "a"):
             for o in range(PASSES):
@@ -142,12 +147,13 @@ def tile_picked_yhnet_grad_p_kernel(
 
         for side in ("b", "a"):
             gather_words(side, 0, 0, ENTRIES)
-        for side in ("b", "a"):
-            gather_scales(side)
+        gather_scales("b")
         for pair in range(2):
             cast_w(0, pair, False)
-        for pair in range(2):
-            quant_w(0, pair)
+        quant_w(0, 0)
+        x_scale["a"] = sb("x_scale_a", [P, ENTRIES], U8, tag="w_bf00")
+        gather_scales("a")
+        quant_w(0, 1)
         for c in range(CHUNKS):
             first_product(0, "b", c, True)
         for pair in range(2):

@@ -73,10 +73,10 @@ def tile_picked_yhnet_grad_p_kernel(
                 )
 
         nc.gpsimd.memset(scale_table[:].bitcast(I32), 0)
-        load_scales(0)
         load_words(0)
         nc.sync.dma_start(list_b[:], other)
         nc.sync.dma_start(list_a[:], offs)
+        load_scales(0)
         load_weights(0)
         load_scales(1)
         load_weights(1)
@@ -113,9 +113,9 @@ def tile_picked_yhnet_grad_p_kernel(
             for o in range(PASSES):
                 x_code[side, o] = sb("x_code_%s%d" % (side, o), [P, ENTRIES], U32)
 
-        def cast_w(o, pair, on_vector):
-            src = w_raw[o][:].rearrange("p j (m pair e) -> p pair m j e", pair=2, e=2)[:, pair]
-            dst = w_bf[o, pair][:].rearrange("p e (m j) -> p m j e", j=PACK)
+        def cast_w(o, pair, on_vector, first_m=0, count=P):
+            src = w_raw[o][:].rearrange("p j (m pair e) -> p pair m j e", pair=2, e=2)[:, pair, first_m : first_m + count]
+            dst = w_bf[o, pair][:].rearrange("p e (m j) -> p m j e", j=PACK)[:, first_m : first_m + count]
             if on_vector:
                 nc.vector.tensor_copy(dst, src)
             else:
@@ -156,8 +156,9 @@ def tile_picked_yhnet_grad_p_kernel(
         quant_w(0, 1)
         for c in range(CHUNKS):
             first_product(0, "b", c, True)
-        for pair in range(2):
-            cast_w(1, pair, pair == 1)
+        cast_w(1, 0, False)
+        cast_w(1, 1, False, 0, P // 2)
+        cast_w(1, 1, True, P // 2, P // 2)
         for pair in range(2):
             quant_w(1, pair)
         for h in range(2):
@@ -222,7 +223,7 @@ def tile_picked_yhnet_grad_p_kernel(
 
         def pieces(c):
             if c == CHUNKS - 1:
-                return [(0, 1), (2, 3)]
+                return [(0, 1, 2), (3,)]
             return [(0, 1, 2, 3)]
 
         def open_total(c):
@@ -294,9 +295,8 @@ def tile_picked_yhnet_grad_p_kernel(
             open_total(c)
         scale_h("b", 0, HALF)
         scale_h("b", HALF, HALF)
-        quant_h("b", 0, HALF)
         scale_h("a", 0, P)
-        quant_h("b", HALF, HALF)
+        quant_h("b", 0, ENTRIES)
         for c in range(CHUNKS):
             if c + 1 < CHUNKS:
                 scale_h("a", P * (c + 1), P)

@@ -28,6 +28,7 @@ BANK = 512
 QUADRANT = 32
 SCALE_ROWS = 4
 FIRST_TURNED = 1
+WARM_UPS = 2
 
 
 def tile_picked_yhnet_grad_p_kernel(
@@ -221,17 +222,25 @@ def tile_picked_yhnet_grad_p_kernel(
             half_tanh[c] = sb("half_tanh%d" % c, [P, V], F32)
             nc.scalar.activation(half_tanh[c][:], y[:], TANH, scale=0.5)
 
+        sim_turned = {}
+        sim_terms = {}
+
+        def turn_sim(c):
+            sim_turned[c] = bank("sim_turned%d" % c, c)
+            for d in range(CHUNKS):
+                nc.tensor.transpose(sim_turned[c][:, block(d)], sim_sb[:, c, block(d)], ident[:])
+
+        def copy_sim(c):
+            sim_terms[c] = sb("sim_term%d" % c, [P, V], F32)
+            nc.scalar.activation(sim_terms[c][:], sim_turned[c][:], COPY, bias=1.0, scale=-2.0)
+
         def pieces(c):
             if c == CHUNKS - 1:
                 return [(0, 1, 2), (3,)]
             return [(0, 1, 2, 3)]
 
         def open_total(c):
-            sim_turned = bank("sim_turned%d" % c, c)
-            for d in range(CHUNKS):
-                nc.tensor.transpose(sim_turned[:, block(d)], sim_sb[:, c, block(d)], ident[:])
-            sim_term = sb("sim_term%d" % c, [P, V], F32)
-            nc.scalar.activation(sim_term[:], sim_turned[:], COPY, bias=1.0, scale=-2.0)
+            sim_term = sim_terms[c]
             for n, piece in enumerate(pieces(c)):
                 total[c, n] = bank("total%d_%d" % (c, n), c + n)
                 for d in piece:
@@ -260,6 +269,9 @@ def tile_picked_yhnet_grad_p_kernel(
             for n, piece in enumerate(pieces(c)):
                 cols = slice(P * piece[0], P * (piece[-1] + 1))
                 nc.scalar.activation(half_tanh[c][:, cols], y[:, cols], TANH, scale=0.5)
+
+        def close_total(c):
+            for n, piece in enumerate(pieces(c)):
                 for d in piece:
                     nc.tensor.matmul(
                         total[c, n][:, block(d)],
@@ -292,7 +304,20 @@ def tile_picked_yhnet_grad_p_kernel(
             for c in range(CHUNKS):
                 steep_tanh(side, c)
         for c in range(FIRST_TURNED, CHUNKS):
-            open_total(c)
+            turn_sim(c)
+        warm = bank("warm", 0)
+        for n in range(WARM_UPS):
+            nc.tensor.matmul_mx(
+                out=warm[:],
+                lhsT=w_code[0, 0][:, block(0)].bitcast(FP8X4),
+                lhsT_scale=w_scale[0, 0][:, block(0)],
+                rhs=x_code["a", 1][:].bitcast(FP8X4),
+                rhs_scale=x_scale["a"][SCALE_ROWS:P, :],
+                start=True,
+                stop=True,
+            )
+        for c in range(FIRST_TURNED, CHUNKS - 1):
+            copy_sim(c)
         scale_h("b", 0, HALF)
         scale_h("b", HALF, HALF)
         scale_h("a", 0, P)
@@ -303,8 +328,12 @@ def tile_picked_yhnet_grad_p_kernel(
             quant_h("a", P * c, P)
             if c < FIRST_TURNED:
                 second_product(c)
+                copy_sim(CHUNKS - 1)
             else:
+                open_total(c)
                 turned_product(c)
+        for c in range(FIRST_TURNED, CHUNKS):
+            close_total(c)
         for c in range(FIRST_TURNED):
             subtract_sim(c)
         for c in range(FIRST_TURNED):

@@ -28,7 +28,7 @@ BANK = 512
 QUADRANT = 32
 SCALE_ROWS = 4
 FIRST_TURNED = 1
-WARM_UPS = 2
+WARM_UPS = 3
 
 
 def tile_picked_yhnet_grad_p_kernel(
@@ -155,8 +155,9 @@ def tile_picked_yhnet_grad_p_kernel(
         x_scale["a"] = sb("x_scale_a", [P, ENTRIES], U8, tag="w_bf00")
         gather_scales("a")
         quant_w(0, 1)
-        for c in range(CHUNKS):
-            first_product(0, "b", c, True)
+        for side in ("b", "a"):
+            for c in range(CHUNKS):
+                first_product(0, side, c, True)
         cast_w(1, 0, False)
         cast_w(1, 1, False, 0, P // 2)
         cast_w(1, 1, True, P // 2, P // 2)
@@ -165,11 +166,9 @@ def tile_picked_yhnet_grad_p_kernel(
         for h in range(2):
             gather_words("b", 1, HALF * h, HALF)
         gather_words("a", 1, 0, ENTRIES)
-        for c in range(CHUNKS):
-            first_product(1, "b", c, False)
-        for c in range(CHUNKS):
-            first_product(1, "a", c, True)
-            first_product(0, "a", c, False)
+        for side in ("b", "a"):
+            for c in range(CHUNKS):
+                first_product(1, side, c, False)
 
         sim_sb = sb("sim_sb", [P, CHUNKS, V], F32, tag="big0")
         wt_sb = sb("wt_sb", [P, CHUNKS, V], F32, tag="big1")
@@ -236,13 +235,13 @@ def tile_picked_yhnet_grad_p_kernel(
 
         def pieces(c):
             if c == CHUNKS - 1:
-                return [(0, 1, 2), (3,)]
+                return [(0, 1, 2, 3)]
             return [(0, 1, 2, 3)]
 
         def open_total(c):
             sim_term = sim_terms[c]
             for n, piece in enumerate(pieces(c)):
-                total[c, n] = bank("total%d_%d" % (c, n), c + n)
+                total[c, n] = bank("total%d_%d" % (c, n), (5, 5)[n] if c == 3 else c)
                 for d in piece:
                     nc.tensor.matmul(
                         total[c, n][:, block(d)],
@@ -283,11 +282,12 @@ def tile_picked_yhnet_grad_p_kernel(
                     )
 
         def finish_total(c):
-            for n, piece in enumerate(pieces(c)):
-                cols = slice(P * piece[0], P * (piece[-1] + 1))
-                res = sb("res%d_%d" % (c, n), [P, cols.stop - cols.start], F32)
+            cuts = (0, V - P, V) if c == CHUNKS - 1 else (0, V)
+            for first, end in zip(cuts, cuts[1:]):
+                cols = slice(first, end)
+                res = sb("res%d_%d" % (c, first), [P, end - first], F32)
                 nc.vector.scalar_tensor_tensor(
-                    res[:], total[c, n][:, cols], 0.5, wt_sb[:, c, cols], ALU.mult, ALU.mult
+                    res[:], total[c, 0][:, cols], 0.5, wt_sb[:, c, cols], ALU.mult, ALU.mult
                 )
                 nc.sync.dma_start(out[block(c), cols], res[:])
 
@@ -322,18 +322,21 @@ def tile_picked_yhnet_grad_p_kernel(
         scale_h("b", HALF, HALF)
         scale_h("a", 0, P)
         quant_h("b", 0, ENTRIES)
-        for c in range(CHUNKS):
+        quant_h("a", 0, P)
+        second_product(0)
+        copy_sim(3)
+        open_total(1)
+        open_total(2)
+        scale_h("a", P, P)
+        for c in range(1, CHUNKS):
             if c + 1 < CHUNKS:
                 scale_h("a", P * (c + 1), P)
             quant_h("a", P * c, P)
-            if c < FIRST_TURNED:
-                second_product(c)
-                copy_sim(CHUNKS - 1)
-            else:
-                open_total(c)
-                turned_product(c)
-        for c in range(FIRST_TURNED, CHUNKS):
-            close_total(c)
+            turned_product(c)
+        close_total(1)
+        open_total(3)
+        close_total(2)
+        close_total(3)
         for c in range(FIRST_TURNED):
             subtract_sim(c)
         for c in range(FIRST_TURNED):

@@ -27,8 +27,12 @@ CHUNKS = ENTRIES // P
 BANK = 512
 QUADRANT = 32
 SCALE_ROWS = 4
-FIRST_TURNED = 1
-WARM_UPS = 3
+PLAIN = 0
+TURNED = (1, 2, 3)
+LAST = CHUNKS - 1
+EARLY_A = 2
+WARM_BANK = CHUNKS + PLAIN
+TOTAL_BANK = {1: 1, 2: 2, 3: CHUNKS + 1}
 
 
 def tile_picked_yhnet_grad_p_kernel(
@@ -115,8 +119,9 @@ def tile_picked_yhnet_grad_p_kernel(
                 x_code[side, o] = sb("x_code_%s%d" % (side, o), [P, ENTRIES], U32)
 
         def cast_w(o, pair, on_vector, first_m=0, count=P):
-            src = w_raw[o][:].rearrange("p j (m pair e) -> p pair m j e", pair=2, e=2)[:, pair, first_m : first_m + count]
-            dst = w_bf[o, pair][:].rearrange("p e (m j) -> p m j e", j=PACK)[:, first_m : first_m + count]
+            ms = slice(first_m, first_m + count)
+            src = w_raw[o][:].rearrange("p j (m pair e) -> p pair m j e", pair=2, e=2)[:, pair, ms]
+            dst = w_bf[o, pair][:].rearrange("p e (m j) -> p m j e", j=PACK)[:, ms]
             if on_vector:
                 nc.vector.tensor_copy(dst, src)
             else:
@@ -155,9 +160,10 @@ def tile_picked_yhnet_grad_p_kernel(
         x_scale["a"] = sb("x_scale_a", [P, ENTRIES], U8, tag="w_bf00")
         gather_scales("a")
         quant_w(0, 1)
-        for side in ("b", "a"):
-            for c in range(CHUNKS):
-                first_product(0, side, c, True)
+        for c in range(CHUNKS):
+            first_product(0, "b", c, True)
+        for c in range(EARLY_A):
+            first_product(0, "a", c, True)
         cast_w(1, 0, False)
         cast_w(1, 1, False, 0, P // 2)
         cast_w(1, 1, True, P // 2, P // 2)
@@ -166,9 +172,12 @@ def tile_picked_yhnet_grad_p_kernel(
         for h in range(2):
             gather_words("b", 1, HALF * h, HALF)
         gather_words("a", 1, 0, ENTRIES)
-        for side in ("b", "a"):
-            for c in range(CHUNKS):
-                first_product(1, side, c, False)
+        for c in range(CHUNKS):
+            first_product(1, "b", c, False)
+        for c in range(CHUNKS):
+            first_product(1, "a", c, c >= EARLY_A)
+            if c >= EARLY_A:
+                first_product(0, "a", c, False)
 
         sim_sb = sb("sim_sb", [P, CHUNKS, V], F32, tag="big0")
         wt_sb = sb("wt_sb", [P, CHUNKS, V], F32, tag="big1")
@@ -204,10 +213,11 @@ def tile_picked_yhnet_grad_p_kernel(
             )
 
         half_tanh = {}
-        diff = {}
+        sim_turned = {}
+        sim_term = {}
         total = {}
 
-        def second_product(c):
+        def plain_product(c):
             y = bank("y%d" % c, c)
             nc.tensor.matmul_mx(
                 out=y[:],
@@ -221,36 +231,32 @@ def tile_picked_yhnet_grad_p_kernel(
             half_tanh[c] = sb("half_tanh%d" % c, [P, V], F32)
             nc.scalar.activation(half_tanh[c][:], y[:], TANH, scale=0.5)
 
-        sim_turned = {}
-        sim_terms = {}
-
         def turn_sim(c):
             sim_turned[c] = bank("sim_turned%d" % c, c)
             for d in range(CHUNKS):
                 nc.tensor.transpose(sim_turned[c][:, block(d)], sim_sb[:, c, block(d)], ident[:])
 
         def copy_sim(c):
-            sim_terms[c] = sb("sim_term%d" % c, [P, V], F32)
-            nc.scalar.activation(sim_terms[c][:], sim_turned[c][:], COPY, bias=1.0, scale=-2.0)
+            sim_term[c] = sb("sim_term%d" % c, [P, V], F32)
+            nc.scalar.activation(sim_term[c][:], sim_turned[c][:], COPY, bias=1.0, scale=-2.0)
 
-        def pieces(c):
-            if c == CHUNKS - 1:
-                return [(0, 1, 2, 3)]
-            return [(0, 1, 2, 3)]
+        def add_turned(c, term, opens):
+            for d in range(CHUNKS):
+                nc.tensor.matmul(
+                    total[c][:, block(d)],
+                    term[:, block(d)],
+                    ident[:],
+                    start=(opens and d == 0),
+                    stop=(not opens and d == CHUNKS - 1),
+                    is_transpose=True,
+                )
 
         def open_total(c):
-            sim_term = sim_terms[c]
-            for n, piece in enumerate(pieces(c)):
-                total[c, n] = bank("total%d_%d" % (c, n), (5, 5)[n] if c == 3 else c)
-                for d in piece:
-                    nc.tensor.matmul(
-                        total[c, n][:, block(d)],
-                        sim_term[:, block(d)],
-                        ident[:],
-                        start=(d == piece[0]),
-                        stop=False,
-                        is_transpose=True,
-                    )
+            total[c] = bank("total%d" % c, TOTAL_BANK[c])
+            add_turned(c, sim_term[c], True)
+
+        def close_total(c):
+            add_turned(c, half_tanh[c], False)
 
         def turned_product(c):
             y = bank("y%d" % c, CHUNKS + c)
@@ -265,81 +271,68 @@ def tile_picked_yhnet_grad_p_kernel(
                     stop=True,
                 )
             half_tanh[c] = sb("half_tanh%d" % c, [P, V], F32)
-            for n, piece in enumerate(pieces(c)):
-                cols = slice(P * piece[0], P * (piece[-1] + 1))
-                nc.scalar.activation(half_tanh[c][:, cols], y[:, cols], TANH, scale=0.5)
+            nc.scalar.activation(half_tanh[c][:], y[:], TANH, scale=0.5)
 
-        def close_total(c):
-            for n, piece in enumerate(pieces(c)):
-                for d in piece:
-                    nc.tensor.matmul(
-                        total[c, n][:, block(d)],
-                        half_tanh[c][:, block(d)],
-                        ident[:],
-                        start=False,
-                        stop=(d == piece[-1]),
-                        is_transpose=True,
-                    )
+        def warm_up(name, still_code, still_scale, moving_code, moving_scale):
+            unread = bank(name, WARM_BANK)
+            nc.tensor.matmul_mx(
+                out=unread[:],
+                lhsT=still_code[:, block(0)].bitcast(FP8X4),
+                lhsT_scale=still_scale[:, block(0)],
+                rhs=moving_code.bitcast(FP8X4),
+                rhs_scale=moving_scale,
+                start=True,
+                stop=True,
+            )
 
-        def finish_total(c):
-            cuts = (0, V - P, V) if c == CHUNKS - 1 else (0, V)
-            for first, end in zip(cuts, cuts[1:]):
-                cols = slice(first, end)
-                res = sb("res%d_%d" % (c, first), [P, end - first], F32)
+        def finish_plain(c):
+            diff = sb("diff", [P, V], F32)
+            res = sb("res%d" % c, [P, V], F32)
+            halves = [slice(0, HALF), slice(HALF, V)]
+            for cols in halves:
                 nc.vector.scalar_tensor_tensor(
-                    res[:], total[c, 0][:, cols], 0.5, wt_sb[:, c, cols], ALU.mult, ALU.mult
+                    diff[:, cols], half_tanh[c][:, cols], 0.5, sim_sb[:, c, cols], ALU.mult, ALU.subtract
                 )
-                nc.sync.dma_start(out[block(c), cols], res[:])
-
-        def subtract_sim(c):
-            diff[c] = sb("diff%d" % c, [P, V], F32)
-            nc.vector.scalar_tensor_tensor(diff[c][:], half_tanh[c][:], 0.5, sim_sb[:, c, :], ALU.mult, ALU.subtract)
-
-        def finish_diff(c):
-            res = sb("res%d_0" % c, [P, V], F32)
-            nc.vector.scalar_tensor_tensor(res[:], diff[c][:], 0.5, wt_sb[:, c, :], ALU.add, ALU.mult)
+            for cols in halves:
+                nc.vector.scalar_tensor_tensor(res[:, cols], diff[:, cols], 0.5, wt_sb[:, c, cols], ALU.add, ALU.mult)
             nc.sync.dma_start(out[block(c), :], res[:])
+
+        def finish_turned(c, cols):
+            res = sb("res%d_%d" % (c, cols.start), [P, cols.stop - cols.start], F32)
+            nc.vector.scalar_tensor_tensor(res[:], total[c][:, cols], 0.5, wt_sb[:, c, cols], ALU.mult, ALU.mult)
+            nc.sync.dma_start(out[block(c), cols], res[:])
 
         for side in ("b", "a"):
             for c in range(CHUNKS):
                 steep_tanh(side, c)
-        for c in range(FIRST_TURNED, CHUNKS):
+        for c in TURNED:
             turn_sim(c)
-        warm = bank("warm", 0)
-        for n in range(WARM_UPS):
-            nc.tensor.matmul_mx(
-                out=warm[:],
-                lhsT=w_code[0, 0][:, block(0)].bitcast(FP8X4),
-                lhsT_scale=w_scale[0, 0][:, block(0)],
-                rhs=x_code["a", 1][:].bitcast(FP8X4),
-                rhs_scale=x_scale["a"][SCALE_ROWS:P, :],
-                start=True,
-                stop=True,
-            )
-        for c in range(FIRST_TURNED, CHUNKS - 1):
+        for name in ("warm0", "warm1"):
+            warm_up(name, w_code[0, 0], w_scale[0, 0], x_code["a", 1][:], x_scale["a"][SCALE_ROWS:P, :])
+        for c in TURNED[:-1]:
             copy_sim(c)
         scale_h("b", 0, HALF)
         scale_h("b", HALF, HALF)
-        scale_h("a", 0, P)
+        scale_h("a", P * PLAIN, P)
         quant_h("b", 0, ENTRIES)
-        quant_h("a", 0, P)
-        second_product(0)
-        copy_sim(3)
-        open_total(1)
-        open_total(2)
-        scale_h("a", P, P)
-        for c in range(1, CHUNKS):
-            if c + 1 < CHUNKS:
+        quant_h("a", P * PLAIN, P)
+        plain_product(PLAIN)
+        warm_up("warm2", h_code["a"], h_scale["a"], h_code["b"][:], h_scale["b"][:])
+        copy_sim(LAST)
+        for c in TURNED[:-1]:
+            open_total(c)
+        scale_h("a", P * TURNED[0], P)
+        for c in TURNED:
+            if c < LAST:
                 scale_h("a", P * (c + 1), P)
             quant_h("a", P * c, P)
             turned_product(c)
-        close_total(1)
-        open_total(3)
-        close_total(2)
-        close_total(3)
-        for c in range(FIRST_TURNED):
-            subtract_sim(c)
-        for c in range(FIRST_TURNED):
-            finish_diff(c)
-        for c in range(FIRST_TURNED, CHUNKS):
-            finish_total(c)
+        close_total(TURNED[0])
+        open_total(LAST)
+        for c in TURNED[1:]:
+            close_total(c)
+        finish_plain(PLAIN)
+        for c in TURNED[:-1]:
+            finish_turned(c, slice(0, V))
+        finish_turned(LAST, slice(0, V - P))
+        finish_turned(LAST, slice(V - P, V))

@@ -30,9 +30,12 @@ SCALE_ROWS = 4
 PLAIN = 0
 TURNED = (1, 2, 3)
 LAST = CHUNKS - 1
-EARLY_A = 2
 WARM_BANK = CHUNKS + PLAIN
-TOTAL_BANK = {1: 1, 2: 2, 3: CHUNKS + 1}
+PIECES = {
+    1: [((0, 1, 2, 3), 1)],
+    2: [((0, 1, 2, 3), 2)],
+    3: [((0, 1, 2), CHUNKS + 1), ((3,), CHUNKS + 2)],
+}
 
 
 def tile_picked_yhnet_grad_p_kernel(
@@ -136,20 +139,25 @@ def tile_picked_yhnet_grad_p_kernel(
 
         z = {}
         for n, side in enumerate(("b", "a")):
-            for c in range(CHUNKS):
-                z[side, c] = bank("z_%s%d" % (side, c), CHUNKS * n + c)
+            for h in range(2):
+                for pair in range(2):
+                    z[side, h, pair] = bank("z_%s%d%d" % (side, h, pair), CHUNKS * n + 2 * h + pair)
 
-        def first_product(o, side, c, opens):
-            for s in range(PACK):
-                nc.tensor.matmul_mx(
-                    out=z[side, c][:, block(s)],
-                    lhsT=w_code[o, s // 2][:, block(s % 2)].bitcast(FP8X4),
-                    lhsT_scale=w_scale[o, s // 2][:, block(s % 2)],
-                    rhs=x_code[side, o][:, block(c)].bitcast(FP8X4),
-                    rhs_scale=x_scale[side][SCALE_ROWS * o : P, block(c)],
-                    start=(opens and s == 0),
-                    stop=(not opens and s == PACK - 1),
-                )
+        def half(h):
+            return slice(HALF * h, HALF * (h + 1))
+
+        def first_product(o, side, h, opens):
+            for pair in range(2):
+                for e in range(2):
+                    nc.tensor.matmul_mx(
+                        out=z[side, h, pair][:, half(e)],
+                        lhsT=w_code[o, pair][:, block(e)].bitcast(FP8X4),
+                        lhsT_scale=w_scale[o, pair][:, block(e)],
+                        rhs=x_code[side, o][:, half(h)].bitcast(FP8X4),
+                        rhs_scale=x_scale[side][SCALE_ROWS * o : P, half(h)],
+                        start=(opens and e == 0),
+                        stop=(not opens and e == 1),
+                    )
 
         for side in ("b", "a"):
             gather_words(side, 0, 0, ENTRIES)
@@ -160,10 +168,9 @@ def tile_picked_yhnet_grad_p_kernel(
         x_scale["a"] = sb("x_scale_a", [P, ENTRIES], U8, tag="w_bf00")
         gather_scales("a")
         quant_w(0, 1)
-        for c in range(CHUNKS):
-            first_product(0, "b", c, True)
-        for c in range(EARLY_A):
-            first_product(0, "a", c, True)
+        for h in range(2):
+            first_product(0, "b", h, True)
+        first_product(0, "a", 0, True)
         cast_w(1, 0, False)
         cast_w(1, 1, False, 0, P // 2)
         cast_w(1, 1, True, P // 2, P // 2)
@@ -172,36 +179,36 @@ def tile_picked_yhnet_grad_p_kernel(
         for h in range(2):
             gather_words("b", 1, HALF * h, HALF)
         gather_words("a", 1, 0, ENTRIES)
-        for c in range(CHUNKS):
-            first_product(1, "b", c, False)
-        for c in range(CHUNKS):
-            first_product(1, "a", c, c >= EARLY_A)
-            if c >= EARLY_A:
-                first_product(0, "a", c, False)
+        for h in range(2):
+            first_product(1, "b", h, False)
+        first_product(1, "a", 0, False)
+        first_product(1, "a", 1, True)
+        first_product(0, "a", 1, False)
 
         sim_sb = sb("sim_sb", [P, CHUNKS, V], F32, tag="big0")
         wt_sb = sb("wt_sb", [P, CHUNKS, V], F32, tag="big1")
         nc.sync.dma_start(sim_sb[:], sim.rearrange("(c p) v -> p c v", p=P))
         nc.sync.dma_start(wt_sb[:], wt.rearrange("(c p) v -> p c v", p=P))
 
-        th = {side: sb("th_" + side, [P, ENTRIES, PACK], F32) for side in ("a", "b")}
+        th = {side: sb("th_" + side, [P, 2, ENTRIES, 2], F32) for side in ("a", "b")}
         h_bf = {side: sb("h_bf_" + side, [P, ENTRIES, PACK], BF16) for side in ("a", "b")}
         h_code = {side: sb("h_code_" + side, [P, ENTRIES], U32) for side in ("a", "b")}
         h_scale = {side: sb("h_scale_" + side, [P, ENTRIES], U8) for side in ("a", "b")}
 
-        def steep_tanh(side, c):
+        def steep_tanh(side, h, pair):
             nc.scalar.activation(
-                th[side][:, block(c), :],
-                z[side, c][:].rearrange("p (s n) -> p n s", s=PACK),
+                th[side][:, pair, half(h), :],
+                z[side, h, pair][:].rearrange("p (e n) -> p n e", e=2),
                 TANH,
                 scale=2.0,
             )
 
         def scale_h(side, first_entry, count):
+            entries = slice(first_entry, first_entry + count)
             nc.vector.tensor_tensor(
-                h_bf[side][:, first_entry : first_entry + count, :],
-                th[side][:, first_entry : first_entry + count, :],
-                factor[side][:].rearrange("p (n s) -> p n s", n=1).to_broadcast([P, count, PACK]),
+                h_bf[side][:, entries, :].rearrange("p n (pair e) -> p n pair e", e=2),
+                th[side][:].rearrange("p pair n e -> p n pair e")[:, entries],
+                factor[side][:].rearrange("p (n pair e) -> p n pair e", n=1, e=2).to_broadcast([P, count, 2, 2]),
                 ALU.mult,
             )
 
@@ -240,23 +247,31 @@ def tile_picked_yhnet_grad_p_kernel(
             sim_term[c] = sb("sim_term%d" % c, [P, V], F32)
             nc.scalar.activation(sim_term[c][:], sim_turned[c][:], COPY, bias=1.0, scale=-2.0)
 
-        def add_turned(c, term, opens):
-            for d in range(CHUNKS):
+        def blocks_of(c):
+            return [piece[0] for piece in PIECES[c]]
+
+        def add_turned(c, blocks, term, opens):
+            for d in blocks:
                 nc.tensor.matmul(
-                    total[c][:, block(d)],
+                    total[c, blocks][:, block(d)],
                     term[:, block(d)],
                     ident[:],
-                    start=(opens and d == 0),
-                    stop=(not opens and d == CHUNKS - 1),
+                    start=(opens and d == blocks[0]),
+                    stop=(not opens and d == blocks[-1]),
                     is_transpose=True,
                 )
 
         def open_total(c):
-            total[c] = bank("total%d" % c, TOTAL_BANK[c])
-            add_turned(c, sim_term[c], True)
+            for blocks, number in PIECES[c]:
+                total[c, blocks] = bank("total%d_%d" % (c, blocks[0]), number)
+                add_turned(c, blocks, sim_term[c], True)
 
         def close_total(c):
-            add_turned(c, half_tanh[c], False)
+            for blocks in blocks_of(c):
+                add_turned(c, blocks, half_tanh[c], False)
+
+        def columns(blocks):
+            return slice(P * blocks[0], P * (blocks[-1] + 1))
 
         def turned_product(c):
             y = bank("y%d" % c, CHUNKS + c)
@@ -271,7 +286,8 @@ def tile_picked_yhnet_grad_p_kernel(
                     stop=True,
                 )
             half_tanh[c] = sb("half_tanh%d" % c, [P, V], F32)
-            nc.scalar.activation(half_tanh[c][:], y[:], TANH, scale=0.5)
+            for blocks in blocks_of(c):
+                nc.scalar.activation(half_tanh[c][:, columns(blocks)], y[:, columns(blocks)], TANH, scale=0.5)
 
         def warm_up(name, still_code, still_scale, moving_code, moving_scale):
             unread = bank(name, WARM_BANK)
@@ -297,14 +313,19 @@ def tile_picked_yhnet_grad_p_kernel(
                 nc.vector.scalar_tensor_tensor(res[:, cols], diff[:, cols], 0.5, wt_sb[:, c, cols], ALU.add, ALU.mult)
             nc.sync.dma_start(out[block(c), :], res[:])
 
-        def finish_turned(c, cols):
-            res = sb("res%d_%d" % (c, cols.start), [P, cols.stop - cols.start], F32)
-            nc.vector.scalar_tensor_tensor(res[:], total[c][:, cols], 0.5, wt_sb[:, c, cols], ALU.mult, ALU.mult)
-            nc.sync.dma_start(out[block(c), cols], res[:])
+        def finish_turned(c):
+            for blocks in blocks_of(c):
+                cols = columns(blocks)
+                res = sb("res%d_%d" % (c, cols.start), [P, cols.stop - cols.start], F32)
+                nc.vector.scalar_tensor_tensor(
+                    res[:], total[c, blocks][:, cols], 0.5, wt_sb[:, c, cols], ALU.mult, ALU.mult
+                )
+                nc.sync.dma_start(out[block(c), cols], res[:])
 
         for side in ("b", "a"):
-            for c in range(CHUNKS):
-                steep_tanh(side, c)
+            for h in range(2):
+                for pair in range(2):
+                    steep_tanh(side, h, pair)
         for c in TURNED:
             turn_sim(c)
         for name in ("warm0", "warm1"):
@@ -332,7 +353,5 @@ def tile_picked_yhnet_grad_p_kernel(
         for c in TURNED[1:]:
             close_total(c)
         finish_plain(PLAIN)
-        for c in TURNED[:-1]:
-            finish_turned(c, slice(0, V))
-        finish_turned(LAST, slice(0, V - P))
-        finish_turned(LAST, slice(V - P, V))
+        for c in TURNED:
+            finish_turned(c)

@@ -72,21 +72,21 @@ def tile_picked_yhnet_grad_p_kernel(
             rows = w1[K_PASS * o : K_PASS * (o + 1), :]
             nc.sync.dma_start(w_raw[o][:], rows.rearrange("(p j) c -> p j c", j=PACK))
 
-        def load_scales(o):
-            for q in range(P // QUADRANT):
-                first = QUADRANT * q + SCALE_ROWS * o
-                nc.sync.dma_start(
-                    scale_table[first : first + SCALE_ROWS, :].bitcast(I32),
-                    x_scales[o, SCALE_ROWS * q : SCALE_ROWS * (q + 1), :].bitcast(I32),
-                )
+        def load_scales(rows):
+            for r in rows:
+                for o in range(PASSES):
+                    nc.sync.dma_start(
+                        scale_table[SCALE_ROWS * o + r : P : QUADRANT, :].bitcast(I32),
+                        x_scales[o, r : SCALE_ROWS * (P // QUADRANT) : SCALE_ROWS, :].bitcast(I32),
+                    )
 
         nc.gpsimd.memset(scale_table[:].bitcast(I32), 0)
         load_words(0)
         nc.sync.dma_start(list_b[:], other)
         nc.sync.dma_start(list_a[:], offs)
-        load_scales(0)
+        load_scales((0, 1))
         load_weights(0)
-        load_scales(1)
+        load_scales((2, 3))
         load_weights(1)
         load_words(1)
         nc.sync.dma_start(factor["b"][:], inv.rearrange("(p s) one -> p (s one)", s=PACK))

@@ -30,7 +30,7 @@ SCALE_ROWS = 4
 PLAIN = 0
 TURNED = (1, 2, 3)
 LAST = CHUNKS - 1
-WARM_BANK = CHUNKS + PLAIN
+WARM_BANK = CHUNKS + 1
 PIECES = {
     1: [((0, 1, 2, 3), 1)],
     2: [((0, 1, 2, 3), 2)],
@@ -54,6 +54,9 @@ def tile_picked_yhnet_grad_p_kernel(
 
         def block(n):
             return slice(P * n, P * (n + 1))
+
+        def half(h):
+            return slice(HALF * h, HALF * (h + 1))
 
         list_a = keep.tile([P, S // 16], U16, name="list_a")
         list_b = keep.tile([P, V // 16], U16, name="list_b")
@@ -110,10 +113,10 @@ def tile_picked_yhnet_grad_p_kernel(
         w_scale = {}
         w_bf = {}
         for o in range(PASSES):
+            w_code[o] = sb("w_code%d" % o, [P, H], U32)
+            w_scale[o] = sb("w_scale%d" % o, [P, H], U8)
             for pair in range(2):
                 w_bf[o, pair] = sb("w_bf%d%d" % (o, pair), [P, 2, P * PACK], BF16)
-                w_code[o, pair] = sb("w_code%d%d" % (o, pair), [P, 2 * P], U32)
-                w_scale[o, pair] = sb("w_scale%d%d" % (o, pair), [P, 2 * P], U8)
 
         x_scale = {"b": sb("x_scale_b", [P, ENTRIES], U8)}
         x_code = {}
@@ -132,8 +135,8 @@ def tile_picked_yhnet_grad_p_kernel(
 
         def quant_w(o, pair):
             nc.vector.quantize_mx(
-                out=w_code[o, pair][:].bitcast(FP8X4),
-                scales=w_scale[o, pair][:],
+                out=w_code[o][:, half(pair)].bitcast(FP8X4),
+                scales=w_scale[o][:, half(pair)],
                 in_=w_bf[o, pair][:].rearrange("p e n -> p (e n)"),
             )
 
@@ -143,16 +146,13 @@ def tile_picked_yhnet_grad_p_kernel(
                 for pair in range(2):
                     z[side, h, pair] = bank("z_%s%d%d" % (side, h, pair), CHUNKS * n + 2 * h + pair)
 
-        def half(h):
-            return slice(HALF * h, HALF * (h + 1))
-
         def first_product(o, side, h, opens):
             for pair in range(2):
                 for e in range(2):
                     nc.tensor.matmul_mx(
                         out=z[side, h, pair][:, half(e)],
-                        lhsT=w_code[o, pair][:, block(e)].bitcast(FP8X4),
-                        lhsT_scale=w_scale[o, pair][:, block(e)],
+                        lhsT=w_code[o][:, block(2 * pair + e)].bitcast(FP8X4),
+                        lhsT_scale=w_scale[o][:, block(2 * pair + e)],
                         rhs=x_code[side, o][:, half(h)].bitcast(FP8X4),
                         rhs_scale=x_scale[side][SCALE_ROWS * o : P, half(h)],
                         start=(opens and e == 0),
@@ -289,14 +289,14 @@ def tile_picked_yhnet_grad_p_kernel(
             for blocks in blocks_of(c):
                 nc.scalar.activation(half_tanh[c][:, columns(blocks)], y[:, columns(blocks)], TANH, scale=0.5)
 
-        def warm_up(name, still_code, still_scale, moving_code, moving_scale):
+        def warm_up(name):
             unread = bank(name, WARM_BANK)
             nc.tensor.matmul_mx(
                 out=unread[:],
-                lhsT=still_code[:, block(0)].bitcast(FP8X4),
-                lhsT_scale=still_scale[:, block(0)],
-                rhs=moving_code.bitcast(FP8X4),
-                rhs_scale=moving_scale,
+                lhsT=w_code[0][:, block(0)].bitcast(FP8X4),
+                lhsT_scale=w_scale[0][:, block(0)],
+                rhs=w_code[1][:].bitcast(FP8X4),
+                rhs_scale=w_scale[1][:],
                 start=True,
                 stop=True,
             )
@@ -329,7 +329,7 @@ def tile_picked_yhnet_grad_p_kernel(
         for c in TURNED:
             turn_sim(c)
         for name in ("warm0", "warm1"):
-            warm_up(name, w_code[0, 0], w_scale[0, 0], x_code["a", 1][:], x_scale["a"][SCALE_ROWS:P, :])
+            warm_up(name)
         for c in TURNED[:-1]:
             copy_sim(c)
         scale_h("b", 0, HALF)
@@ -338,7 +338,6 @@ def tile_picked_yhnet_grad_p_kernel(
         quant_h("b", 0, ENTRIES)
         quant_h("a", P * PLAIN, P)
         plain_product(PLAIN)
-        warm_up("warm2", h_code["a"], h_scale["a"], h_code["b"][:], h_scale["b"][:])
         copy_sim(LAST)
         for c in TURNED[:-1]:
             open_total(c)

@@ -27,14 +27,18 @@ CHUNKS = ENTRIES // P
 BANK = 512
 QUADRANT = 32
 SCALE_ROWS = 4
-PLAIN = 0
-TURNED = (1, 2, 3)
 LAST = CHUNKS - 1
-WARM_BANK = CHUNKS + 1
+ORDER = (0, 1, 2, 3)
+A, B, C, D = ORDER
+Z_CHUNK = {"b": (0, 1), "a": {A: 4, B: 5, C: 0, D: 6}}
+Z_PAIR = (2, 3)
+SIM_BANK = {B: 6, C: 7, D: 2}
+Y_BANK = {A: 5, B: 1, C: 7, D: 0}
 PIECES = {
-    1: [((0, 1, 2, 3), 1)],
-    2: [((0, 1, 2, 3), 2)],
-    3: [((0, 1, 2), CHUNKS + 1), ((3,), CHUNKS + 2)],
+    A: [((0, 1, 2, 3), None)],
+    B: [((0, 1, 2, 3), 3)],
+    C: [((0, 1, 2, 3), 4)],
+    D: [((0, 1, 2), 2), ((3,), 6)],
 }
 
 
@@ -140,24 +144,31 @@ def tile_picked_yhnet_grad_p_kernel(
                 in_=w_bf[o, pair][:].rearrange("p e n -> p (e n)"),
             )
 
-        z = {}
-        for n, side in enumerate(("b", "a")):
-            for h in range(2):
-                for pair in range(2):
-                    z[side, h, pair] = bank("z_%s%d%d" % (side, h, pair), CHUNKS * n + 2 * h + pair)
+        def z_pass(dst, o, slot, side, cols, start, stop):
+            nc.tensor.matmul_mx(
+                out=dst,
+                lhsT=w_code[o][:, block(slot)].bitcast(FP8X4),
+                lhsT_scale=w_scale[o][:, block(slot)],
+                rhs=x_code[side, o][:, cols].bitcast(FP8X4),
+                rhs_scale=x_scale[side][SCALE_ROWS * o : P, cols],
+                start=start,
+                stop=stop,
+            )
 
-        def first_product(o, side, h, opens):
+        z = {}
+
+        def chunk_product(o, side, c, opens):
+            if opens:
+                z[side, c] = bank("z_%s%d" % (side, c), Z_CHUNK[side][c])
+            for slot in range(PACK):
+                z_pass(z[side, c][:, block(slot)], o, slot, side, block(c), opens and slot == 0, not opens and slot == PACK - 1)
+
+        def pair_product(o, opens):
             for pair in range(2):
+                if opens:
+                    z["pair", pair] = bank("z_bp%d" % pair, Z_PAIR[pair])
                 for e in range(2):
-                    nc.tensor.matmul_mx(
-                        out=z[side, h, pair][:, half(e)],
-                        lhsT=w_code[o][:, block(2 * pair + e)].bitcast(FP8X4),
-                        lhsT_scale=w_scale[o][:, block(2 * pair + e)],
-                        rhs=x_code[side, o][:, half(h)].bitcast(FP8X4),
-                        rhs_scale=x_scale[side][SCALE_ROWS * o : P, half(h)],
-                        start=(opens and e == 0),
-                        stop=(not opens and e == 1),
-                    )
+                    z_pass(z["pair", pair][:, half(e)], o, 2 * pair + e, "b", half(1), opens and e == 0, not opens and e == 1)
 
         for side in ("b", "a"):
             gather_words(side, 0, 0, ENTRIES)
@@ -168,49 +179,62 @@ def tile_picked_yhnet_grad_p_kernel(
         x_scale["a"] = sb("x_scale_a", [P, ENTRIES], U8, tag="w_bf00")
         gather_scales("a")
         quant_w(0, 1)
-        for h in range(2):
-            first_product(0, "b", h, True)
-        first_product(0, "a", 0, True)
+        for c in range(2):
+            chunk_product(0, "b", c, True)
+        pair_product(0, True)
+        for c in ORDER[:2]:
+            chunk_product(0, "a", c, True)
         cast_w(1, 0, False)
         cast_w(1, 1, False, 0, P // 2)
         cast_w(1, 1, True, P // 2, P // 2)
         for pair in range(2):
             quant_w(1, pair)
-        for h in range(2):
-            gather_words("b", 1, HALF * h, HALF)
+        gather_words("b", 1, 0, P)
+        gather_words("b", 1, P, P)
+        gather_words("b", 1, HALF, HALF)
         gather_words("a", 1, 0, ENTRIES)
-        for h in range(2):
-            first_product(1, "b", h, False)
-        first_product(1, "a", 0, False)
-        first_product(1, "a", 1, True)
-        first_product(0, "a", 1, False)
+        for c in range(2):
+            chunk_product(1, "b", c, False)
+        pair_product(1, False)
 
         sim_sb = sb("sim_sb", [P, CHUNKS, V], F32, tag="big0")
         wt_sb = sb("wt_sb", [P, CHUNKS, V], F32, tag="big1")
-        nc.sync.dma_start(sim_sb[:], sim.rearrange("(c p) v -> p c v", p=P))
+        for first, count in ((1, CHUNKS - 1), (0, 1)):
+            rows = sim[P * first : P * (first + count), :]
+            nc.sync.dma_start(sim_sb[:, first : first + count, :], rows.rearrange("(c p) v -> p c v", p=P))
         nc.sync.dma_start(wt_sb[:], wt.rearrange("(c p) v -> p c v", p=P))
 
-        th = {side: sb("th_" + side, [P, 2, ENTRIES, 2], F32) for side in ("a", "b")}
+        th_b = [sb("th_b%d" % h, [P, 2, HALF, 2], F32) for h in range(2)]
+        th_a = [sb("th_a%d" % c, [P, 2, P, 2], F32) for c in range(CHUNKS)]
         h_bf = {side: sb("h_bf_" + side, [P, ENTRIES, PACK], BF16) for side in ("a", "b")}
         h_code = {side: sb("h_code_" + side, [P, ENTRIES], U32) for side in ("a", "b")}
         h_scale = {side: sb("h_scale_" + side, [P, ENTRIES], U8) for side in ("a", "b")}
 
-        def steep_tanh(side, h, pair):
-            nc.scalar.activation(
-                th[side][:, pair, half(h), :],
-                z[side, h, pair][:].rearrange("p (e n) -> p n e", e=2),
-                TANH,
-                scale=2.0,
-            )
+        def tanh_chunk(dst, src):
+            nc.scalar.activation(dst, src[:].rearrange("p (pair e n) -> p pair n e", pair=2, e=2), TANH, scale=2.0)
 
-        def scale_h(side, first_entry, count):
+        def tanh_b():
+            for c in range(2):
+                tanh_chunk(th_b[0][:, :, block(c), :], z["b", c])
+            for pair in range(2):
+                nc.scalar.activation(
+                    th_b[1][:, pair], z["pair", pair][:].rearrange("p (e n) -> p n e", e=2), TANH, scale=2.0
+                )
+
+        def tanh_a(c):
+            tanh_chunk(th_a[c][:], z["a", c])
+
+        def scale_h(side, th, first_entry, count):
             entries = slice(first_entry, first_entry + count)
             nc.vector.tensor_tensor(
                 h_bf[side][:, entries, :].rearrange("p n (pair e) -> p n pair e", e=2),
-                th[side][:].rearrange("p pair n e -> p n pair e")[:, entries],
+                th[:].rearrange("p pair n e -> p n pair e"),
                 factor[side][:].rearrange("p (n pair e) -> p n pair e", n=1, e=2).to_broadcast([P, count, 2, 2]),
                 ALU.mult,
             )
+
+        def scale_a(c):
+            scale_h("a", th_a[c], P * c, P)
 
         def quant_h(side, first_entry, count):
             nc.vector.quantize_mx(
@@ -219,27 +243,17 @@ def tile_picked_yhnet_grad_p_kernel(
                 in_=h_bf[side][:, first_entry : first_entry + count, :].rearrange("p n s -> p (n s)"),
             )
 
+        def quant_a(c):
+            quant_h("a", P * c, P)
+
         half_tanh = {}
         sim_turned = {}
         sim_term = {}
         total = {}
-
-        def plain_product(c):
-            y = bank("y%d" % c, c)
-            nc.tensor.matmul_mx(
-                out=y[:],
-                lhsT=h_code["a"][:, block(c)].bitcast(FP8X4),
-                lhsT_scale=h_scale["a"][:, block(c)],
-                rhs=h_code["b"][:].bitcast(FP8X4),
-                rhs_scale=h_scale["b"][:],
-                start=True,
-                stop=True,
-            )
-            half_tanh[c] = sb("half_tanh%d" % c, [P, V], F32)
-            nc.scalar.activation(half_tanh[c][:], y[:], TANH, scale=0.5)
+        y = {}
 
         def turn_sim(c):
-            sim_turned[c] = bank("sim_turned%d" % c, c)
+            sim_turned[c] = bank("sim_turned%d" % c, SIM_BANK[c])
             for d in range(CHUNKS):
                 nc.tensor.transpose(sim_turned[c][:, block(d)], sim_sb[:, c, block(d)], ident[:])
 
@@ -247,10 +261,10 @@ def tile_picked_yhnet_grad_p_kernel(
             sim_term[c] = sb("sim_term%d" % c, [P, V], F32)
             nc.scalar.activation(sim_term[c][:], sim_turned[c][:], COPY, bias=1.0, scale=-2.0)
 
-        def blocks_of(c):
-            return [piece[0] for piece in PIECES[c]]
-
-        def add_turned(c, blocks, term, opens):
+        def add_turned(c, piece, term, opens):
+            blocks, number = piece
+            if opens:
+                total[c, blocks] = bank("total%d_%d" % (c, blocks[0]), number)
             for d in blocks:
                 nc.tensor.matmul(
                     total[c, blocks][:, block(d)],
@@ -262,22 +276,21 @@ def tile_picked_yhnet_grad_p_kernel(
                 )
 
         def open_total(c):
-            for blocks, number in PIECES[c]:
-                total[c, blocks] = bank("total%d_%d" % (c, blocks[0]), number)
-                add_turned(c, blocks, sim_term[c], True)
+            for piece in PIECES[c]:
+                add_turned(c, piece, sim_term[c], True)
 
         def close_total(c):
-            for blocks in blocks_of(c):
-                add_turned(c, blocks, half_tanh[c], False)
+            for piece in PIECES[c]:
+                add_turned(c, piece, half_tanh[c], False)
 
         def columns(blocks):
             return slice(P * blocks[0], P * (blocks[-1] + 1))
 
-        def turned_product(c):
-            y = bank("y%d" % c, CHUNKS + c)
+        def second_product(c):
+            y[c] = bank("y%d" % c, Y_BANK[c])
             for d in range(CHUNKS):
                 nc.tensor.matmul_mx(
-                    out=y[:, block(d)],
+                    out=y[c][:, block(d)],
                     lhsT=h_code["b"][:, block(d)].bitcast(FP8X4),
                     lhsT_scale=h_scale["b"][:, block(d)],
                     rhs=h_code["a"][:, block(c)].bitcast(FP8X4),
@@ -285,18 +298,15 @@ def tile_picked_yhnet_grad_p_kernel(
                     start=True,
                     stop=True,
                 )
-            half_tanh[c] = sb("half_tanh%d" % c, [P, V], F32)
-            for blocks in blocks_of(c):
-                nc.scalar.activation(half_tanh[c][:, columns(blocks)], y[:, columns(blocks)], TANH, scale=0.5)
 
-        def warm_up(name):
-            unread = bank(name, WARM_BANK)
+        def plain_product(c):
+            y[c] = bank("y%d" % c, Y_BANK[c])
             nc.tensor.matmul_mx(
-                out=unread[:],
-                lhsT=w_code[0][:, block(0)].bitcast(FP8X4),
-                lhsT_scale=w_scale[0][:, block(0)],
-                rhs=w_code[1][:].bitcast(FP8X4),
-                rhs_scale=w_scale[1][:],
+                out=y[c][:],
+                lhsT=h_code["a"][:, block(c)].bitcast(FP8X4),
+                lhsT_scale=h_scale["a"][:, block(c)],
+                rhs=h_code["b"][:].bitcast(FP8X4),
+                rhs_scale=h_scale["b"][:],
                 start=True,
                 stop=True,
             )
@@ -313,8 +323,13 @@ def tile_picked_yhnet_grad_p_kernel(
                 nc.vector.scalar_tensor_tensor(res[:, cols], diff[:, cols], 0.5, wt_sb[:, c, cols], ALU.add, ALU.mult)
             nc.sync.dma_start(out[block(c), :], res[:])
 
-        def finish_turned(c):
-            for blocks in blocks_of(c):
+        def tanh_y(c):
+            half_tanh[c] = sb("half_tanh%d" % c, [P, V], F32)
+            for blocks, number in PIECES[c]:
+                nc.scalar.activation(half_tanh[c][:, columns(blocks)], y[c][:, columns(blocks)], TANH, scale=0.5)
+
+        def finish(c):
+            for blocks, number in PIECES[c]:
                 cols = columns(blocks)
                 res = sb("res%d_%d" % (c, cols.start), [P, cols.stop - cols.start], F32)
                 nc.vector.scalar_tensor_tensor(
@@ -322,35 +337,46 @@ def tile_picked_yhnet_grad_p_kernel(
                 )
                 nc.sync.dma_start(out[block(c), cols], res[:])
 
-        for side in ("b", "a"):
-            for h in range(2):
-                for pair in range(2):
-                    steep_tanh(side, h, pair)
-        for c in TURNED:
-            turn_sim(c)
-        for name in ("warm0", "warm1"):
-            warm_up(name)
-        for c in TURNED[:-1]:
-            copy_sim(c)
-        scale_h("b", 0, HALF)
-        scale_h("b", HALF, HALF)
-        scale_h("a", P * PLAIN, P)
+        turn_sim(B)
+        for c in (A, B):
+            chunk_product(1, "a", c, False)
+        turn_sim(C)
+        tanh_b()
+        for c in (C, D):
+            chunk_product(1, "a", c, True)
+            chunk_product(0, "a", c, False)
+        turn_sim(D)
+        tanh_a(A)
+        tanh_a(B)
+        copy_sim(B)
+        copy_sim(C)
+        open_total(B)
+        open_total(C)
+        tanh_a(C)
+        tanh_a(D)
+        copy_sim(D)
+        for h in range(2):
+            scale_h("b", th_b[h], HALF * h, HALF)
+        scale_a(A)
+        scale_a(B)
         quant_h("b", 0, ENTRIES)
-        quant_h("a", P * PLAIN, P)
-        plain_product(PLAIN)
-        copy_sim(LAST)
-        for c in TURNED[:-1]:
-            open_total(c)
-        scale_h("a", P * TURNED[0], P)
-        for c in TURNED:
-            if c < LAST:
-                scale_h("a", P * (c + 1), P)
-            quant_h("a", P * c, P)
-            turned_product(c)
-        close_total(TURNED[0])
-        open_total(LAST)
-        for c in TURNED[1:]:
-            close_total(c)
-        finish_plain(PLAIN)
-        for c in TURNED:
-            finish_turned(c)
+        quant_h("a", 0, HALF)
+        plain_product(A)
+        second_product(B)
+        open_total(D)
+        tanh_y(A)
+        tanh_y(B)
+        scale_a(C)
+        scale_a(D)
+        quant_a(C)
+        quant_a(D)
+        second_product(C)
+        second_product(D)
+        close_total(B)
+        tanh_y(C)
+        tanh_y(D)
+        close_total(C)
+        close_total(D)
+        finish_plain(A)
+        for c in (B, C, D):
+            finish(c)

@@ -34,6 +34,7 @@ Z_CHUNK = {"b": (0, 1), "a": {A: 4, B: 5, C: 0, D: 6}}
 Z_PAIR = (2, 3)
 SIM_BANK = {B: 6, C: 7, D: 2}
 Y_BANK = {A: 5, B: 1, C: 7, D: 0}
+TANH_PIECES = {A: [(0, 1, 2, 3)], B: [(0, 1, 2, 3)], C: [(0, 1), (2, 3)], D: [(0, 1, 2), (3,)]}
 PIECES = {
     A: [((0, 1, 2, 3), None)],
     B: [((0, 1, 2, 3), 3)],
@@ -325,7 +326,7 @@ def tile_picked_yhnet_grad_p_kernel(
 
         def tanh_y(c):
             half_tanh[c] = sb("half_tanh%d" % c, [P, V], F32)
-            for blocks, number in PIECES[c]:
+            for blocks in TANH_PIECES[c]:
                 nc.scalar.activation(half_tanh[c][:, columns(blocks)], y[c][:, columns(blocks)], TANH, scale=0.5)
 
         def finish(c):

@@ -1,7 +1,6 @@
 from contextlib import ExitStack
 
 import concourse.mybir as mybir
-from concourse.masks import make_identity
 
 K, T, S, H, V = 1024, 2048, 512, 512, 512
 FLOPS = 2 * K * H * (S + V) + 2 * H * S * V
@@ -27,20 +26,7 @@ CHUNKS = ENTRIES // P
 BANK = 512
 QUADRANT = 32
 SCALE_ROWS = 4
-LAST = CHUNKS - 1
-ORDER = (0, 1, 2, 3)
-A, B, C, D = ORDER
-Z_CHUNK = {"b": (0, 1), "a": {A: 4, B: 5, C: 0, D: 6}}
-Z_PAIR = (2, 3)
-SIM_BANK = {B: 6, C: 7, D: 2}
-Y_BANK = {A: 5, B: 1, C: 7, D: 0}
-TANH_PIECES = {A: [(0, 1, 2, 3)], B: [(0, 1, 2, 3)], C: [(0, 1), (2, 3)], D: [(0, 1, 2), (3,)]}
-PIECES = {
-    A: [((0, 1, 2, 3), None)],
-    B: [((0, 1, 2, 3), 3)],
-    C: [((0, 1, 2, 3), 4)],
-    D: [((0, 1, 2), 2), ((3,), 6)],
-}
+A, B, C, D = range(CHUNKS)
 
 
 def tile_picked_yhnet_grad_p_kernel(
@@ -63,12 +49,28 @@ def tile_picked_yhnet_grad_p_kernel(
         def half(h):
             return slice(HALF * h, HALF * (h + 1))
 
-        list_a = keep.tile([P, S // 16], U16, name="list_a")
-        list_b = keep.tile([P, V // 16], U16, name="list_b")
+        def columns(blocks):
+            return slice(P * blocks[0], P * (blocks[-1] + 1))
+
+        lists = {side: keep.tile([P, ENTRIES // 16], U16, name="list_" + side) for side in ("b", "a")}
         word_table = [sb("word_table%d" % o, [P, T], U32) for o in range(PASSES)]
-        w_raw = [sb("w_raw%d" % o, [P, PACK, H], F32, tag="big%d" % o) for o in range(PASSES)]
         scale_table = sb("scale_table", [P, T], U8)
         factor = {side: sb("factor_" + side, [P, PACK], F32) for side in ("b", "a")}
+
+        nc.gpsimd.memset(scale_table[:].bitcast(I32), 0)
+        ident = sb("ident", [P, P], F32)
+        zeros = sb("zeros", [P, P], F32)
+        nc.gpsimd.memset(zeros[:], 0.0)
+        nc.gpsimd.affine_select(
+            out=ident[:],
+            in_=zeros[:],
+            compare_op=ALU.not_equal,
+            fill=1.0,
+            base=0,
+            pattern=[[-1, P]],
+            channel_multiplier=1,
+        )
+        w_raw = [sb("w_raw%d" % o, [P, PACK, H], F32, tag="big%d" % o) for o in range(PASSES)]
 
         def load_words(o):
             nc.sync.dma_start(
@@ -80,63 +82,45 @@ def tile_picked_yhnet_grad_p_kernel(
             rows = w1[K_PASS * o : K_PASS * (o + 1), :]
             nc.sync.dma_start(w_raw[o][:], rows.rearrange("(p j) c -> p j c", j=PACK))
 
-        def load_scales(rows):
+        def load_scales(queue, rows):
             for r in rows:
                 for o in range(PASSES):
-                    nc.sync.dma_start(
+                    queue.dma_start(
                         scale_table[SCALE_ROWS * o + r : P : QUADRANT, :].bitcast(I32),
                         x_scales[o, r : SCALE_ROWS * (P // QUADRANT) : SCALE_ROWS, :].bitcast(I32),
                     )
 
-        nc.gpsimd.memset(scale_table[:].bitcast(I32), 0)
         load_words(0)
-        nc.sync.dma_start(list_b[:], other)
-        nc.sync.dma_start(list_a[:], offs)
-        load_scales((0, 1))
+        nc.sync.dma_start(lists["b"][:], other)
+        nc.sync.dma_start(lists["a"][:], offs)
+        load_scales(nc.sync, (0, 1))
         load_weights(0)
-        load_scales((2, 3))
+        load_scales(nc.sync, (2, 3))
         load_weights(1)
         load_words(1)
         nc.sync.dma_start(factor["b"][:], inv.rearrange("(p s) one -> p (s one)", s=PACK))
         nc.sync.dma_start(factor["a"][:], unit.rearrange("(p s) one -> p (s one)", s=PACK))
 
-        ident = sb("ident", [P, P], F32)
-        make_identity(nc, ident[:])
+        w_code = [sb("w_code%d" % o, [P, H], U32) for o in range(PASSES)]
+        w_scale = [sb("w_scale%d" % o, [P, H], U8) for o in range(PASSES)]
+        w_bf = {(o, pair): sb("w_bf%d%d" % (o, pair), [P, 2, K_PASS], BF16) for o in range(PASSES) for pair in range(2)}
+        x_code = {(side, o): sb("x_code_%s%d" % (side, o), [P, ENTRIES], U32) for side in "ba" for o in range(PASSES)}
+        x_scale = {"b": sb("x_scale_b", [P, ENTRIES], U8)}
 
-        lists = {"a": list_a, "b": list_b}
-
-        def gather_words(side, o, first_entry, count):
+        def gather_words(side, o, first, count):
             nc.vector.tensor_copy(
-                x_code[side, o][:, first_entry : first_entry + count],
-                word_table[o][:].indirect(lists[side][:, first_entry // 16 : (first_entry + count) // 16]),
+                x_code[side, o][:, first : first + count],
+                word_table[o][:].indirect(lists[side][:, first // 16 : (first + count) // 16]),
             )
 
         def gather_scales(side):
             nc.vector.tensor_copy(x_scale[side][:], scale_table[:].indirect(lists[side][:]))
 
-        w_code = {}
-        w_scale = {}
-        w_bf = {}
-        for o in range(PASSES):
-            w_code[o] = sb("w_code%d" % o, [P, H], U32)
-            w_scale[o] = sb("w_scale%d" % o, [P, H], U8)
-            for pair in range(2):
-                w_bf[o, pair] = sb("w_bf%d%d" % (o, pair), [P, 2, P * PACK], BF16)
-
-        x_scale = {"b": sb("x_scale_b", [P, ENTRIES], U8)}
-        x_code = {}
-        for side in ("b", "a"):
-            for o in range(PASSES):
-                x_code[side, o] = sb("x_code_%s%d" % (side, o), [P, ENTRIES], U32)
-
-        def cast_w(o, pair, on_vector, first_m=0, count=P):
+        def cast_w(o, pair, copy, first_m=0, count=P):
             ms = slice(first_m, first_m + count)
             src = w_raw[o][:].rearrange("p j (m pair e) -> p pair m j e", pair=2, e=2)[:, pair, ms]
             dst = w_bf[o, pair][:].rearrange("p e (m j) -> p m j e", j=PACK)[:, ms]
-            if on_vector:
-                nc.vector.tensor_copy(dst, src)
-            else:
-                nc.scalar.copy(dst, src)
+            copy(dst, src)
 
         def quant_w(o, pair):
             nc.vector.quantize_mx(
@@ -158,45 +142,46 @@ def tile_picked_yhnet_grad_p_kernel(
 
         z = {}
 
-        def chunk_product(o, side, c, opens):
+        def chunk_product(o, side, c, number=None):
+            opens = number is not None
             if opens:
-                z[side, c] = bank("z_%s%d" % (side, c), Z_CHUNK[side][c])
+                z[side, c] = bank("z_%s%d" % (side, c), number)
             for slot in range(PACK):
                 z_pass(z[side, c][:, block(slot)], o, slot, side, block(c), opens and slot == 0, not opens and slot == PACK - 1)
 
-        def pair_product(o, opens):
+        def half_product(o, side, h, numbers=None):
+            opens = numbers is not None
             for pair in range(2):
                 if opens:
-                    z["pair", pair] = bank("z_bp%d" % pair, Z_PAIR[pair])
+                    z[side, h, pair] = bank("z_%s%d%d" % (side, h, pair), numbers[pair])
                 for e in range(2):
-                    z_pass(z["pair", pair][:, half(e)], o, 2 * pair + e, "b", half(1), opens and e == 0, not opens and e == 1)
+                    z_pass(z[side, h, pair][:, half(e)], o, 2 * pair + e, side, half(h), opens and e == 0, not opens and e == 1)
 
-        for side in ("b", "a"):
+        for side in "ba":
             gather_words(side, 0, 0, ENTRIES)
         gather_scales("b")
         for pair in range(2):
-            cast_w(0, pair, False)
+            cast_w(0, pair, nc.scalar.copy)
         quant_w(0, 0)
         x_scale["a"] = sb("x_scale_a", [P, ENTRIES], U8, tag="w_bf00")
         gather_scales("a")
         quant_w(0, 1)
-        for c in range(2):
-            chunk_product(0, "b", c, True)
-        pair_product(0, True)
-        for c in ORDER[:2]:
-            chunk_product(0, "a", c, True)
-        cast_w(1, 0, False)
-        cast_w(1, 1, False, 0, P // 2)
-        cast_w(1, 1, True, P // 2, P // 2)
-        for pair in range(2):
-            quant_w(1, pair)
+        chunk_product(0, "b", 0, 0)
+        chunk_product(0, "b", 1, 1)
+        half_product(0, "b", 1, (2, 3))
+        half_product(0, "a", 0, (4, 5))
+        cast_w(1, 0, nc.scalar.copy)
+        cast_w(1, 1, nc.scalar.copy, 0, P // 2)
+        cast_w(1, 1, nc.vector.tensor_copy, P // 2, P // 2)
+        quant_w(1, 0)
+        quant_w(1, 1)
         gather_words("b", 1, 0, P)
         gather_words("b", 1, P, P)
         gather_words("b", 1, HALF, HALF)
         gather_words("a", 1, 0, ENTRIES)
-        for c in range(2):
-            chunk_product(1, "b", c, False)
-        pair_product(1, False)
+        chunk_product(1, "b", 0)
+        chunk_product(1, "b", 1)
+        half_product(1, "b", 1)
 
         sim_sb = sb("sim_sb", [P, CHUNKS, V], F32, tag="big0")
         wt_sb = sb("wt_sb", [P, CHUNKS, V], F32, tag="big1")
@@ -205,47 +190,39 @@ def tile_picked_yhnet_grad_p_kernel(
             nc.sync.dma_start(sim_sb[:, first : first + count, :], rows.rearrange("(c p) v -> p c v", p=P))
         nc.sync.dma_start(wt_sb[:], wt.rearrange("(c p) v -> p c v", p=P))
 
-        th_b = [sb("th_b%d" % h, [P, 2, HALF, 2], F32) for h in range(2)]
-        th_a = [sb("th_a%d" % c, [P, 2, P, 2], F32) for c in range(CHUNKS)]
-        h_bf = {side: sb("h_bf_" + side, [P, ENTRIES, PACK], BF16) for side in ("a", "b")}
-        h_code = {side: sb("h_code_" + side, [P, ENTRIES], U32) for side in ("a", "b")}
-        h_scale = {side: sb("h_scale_" + side, [P, ENTRIES], U8) for side in ("a", "b")}
+        th = {}
+        h_bf = {side: sb("h_bf_" + side, [P, ENTRIES, PACK], BF16) for side in "ab"}
+        h_code = {side: sb("h_code_" + side, [P, ENTRIES], U32) for side in "ab"}
+        h_scale = {side: sb("h_scale_" + side, [P, ENTRIES], U8) for side in "ab"}
 
-        def tanh_chunk(dst, src):
-            nc.scalar.activation(dst, src[:].rearrange("p (pair e n) -> p pair n e", pair=2, e=2), TANH, scale=2.0)
+        def th_tile(side, first, count):
+            th[side, first] = sb("th_%s%d" % (side, first), [P, 2, count, 2], F32)
+            return th[side, first]
 
-        def tanh_b():
-            for c in range(2):
-                tanh_chunk(th_b[0][:, :, block(c), :], z["b", c])
+        def tanh_chunk(dst, side, c):
+            src = z[side, c][:].rearrange("p (pair e n) -> p pair n e", pair=2, e=2)
+            nc.scalar.activation(dst, src, TANH, scale=2.0)
+
+        def tanh_half(side, h):
+            dst = th_tile(side, HALF * h, HALF)
             for pair in range(2):
-                nc.scalar.activation(
-                    th_b[1][:, pair], z["pair", pair][:].rearrange("p (e n) -> p n e", e=2), TANH, scale=2.0
-                )
+                src = z[side, h, pair][:].rearrange("p (e n) -> p n e", e=2)
+                nc.scalar.activation(dst[:, pair], src, TANH, scale=2.0)
 
-        def tanh_a(c):
-            tanh_chunk(th_a[c][:], z["a", c])
-
-        def scale_h(side, th, first_entry, count):
-            entries = slice(first_entry, first_entry + count)
+        def scale_h(side, first, count):
             nc.vector.tensor_tensor(
-                h_bf[side][:, entries, :].rearrange("p n (pair e) -> p n pair e", e=2),
-                th[:].rearrange("p pair n e -> p n pair e"),
+                h_bf[side][:, first : first + count, :].rearrange("p n (pair e) -> p n pair e", e=2),
+                th[side, first][:].rearrange("p pair n e -> p n pair e"),
                 factor[side][:].rearrange("p (n pair e) -> p n pair e", n=1, e=2).to_broadcast([P, count, 2, 2]),
                 ALU.mult,
             )
 
-        def scale_a(c):
-            scale_h("a", th_a[c], P * c, P)
-
-        def quant_h(side, first_entry, count):
+        def quant_h(side, first, count):
             nc.vector.quantize_mx(
-                out=h_code[side][:, first_entry : first_entry + count].bitcast(FP8X4),
-                scales=h_scale[side][:, first_entry : first_entry + count],
-                in_=h_bf[side][:, first_entry : first_entry + count, :].rearrange("p n s -> p (n s)"),
+                out=h_code[side][:, first : first + count].bitcast(FP8X4),
+                scales=h_scale[side][:, first : first + count],
+                in_=h_bf[side][:, first : first + count, :].rearrange("p n s -> p (n s)"),
             )
-
-        def quant_a(c):
-            quant_h("a", P * c, P)
 
         half_tanh = {}
         sim_turned = {}
@@ -253,8 +230,8 @@ def tile_picked_yhnet_grad_p_kernel(
         total = {}
         y = {}
 
-        def turn_sim(c):
-            sim_turned[c] = bank("sim_turned%d" % c, SIM_BANK[c])
+        def turn_sim(c, number):
+            sim_turned[c] = bank("sim_turned%d" % c, number)
             for d in range(CHUNKS):
                 nc.tensor.transpose(sim_turned[c][:, block(d)], sim_sb[:, c, block(d)], ident[:])
 
@@ -262,10 +239,7 @@ def tile_picked_yhnet_grad_p_kernel(
             sim_term[c] = sb("sim_term%d" % c, [P, V], F32)
             nc.scalar.activation(sim_term[c][:], sim_turned[c][:], COPY, bias=1.0, scale=-2.0)
 
-        def add_turned(c, piece, term, opens):
-            blocks, number = piece
-            if opens:
-                total[c, blocks] = bank("total%d_%d" % (c, blocks[0]), number)
+        def add_turned(c, blocks, term, opens):
             for d in blocks:
                 nc.tensor.matmul(
                     total[c, blocks][:, block(d)],
@@ -276,108 +250,100 @@ def tile_picked_yhnet_grad_p_kernel(
                     is_transpose=True,
                 )
 
-        def open_total(c):
-            for piece in PIECES[c]:
-                add_turned(c, piece, sim_term[c], True)
+        def open_total(c, blocks, number):
+            total[c, blocks] = bank("total%d_%d" % (c, blocks[0]), number)
+            add_turned(c, blocks, sim_term[c], True)
 
-        def close_total(c):
-            for piece in PIECES[c]:
-                add_turned(c, piece, half_tanh[c], False)
+        def close_total(c, blocks):
+            add_turned(c, blocks, half_tanh[c], False)
 
-        def columns(blocks):
-            return slice(P * blocks[0], P * (blocks[-1] + 1))
-
-        def second_product(c):
-            y[c] = bank("y%d" % c, Y_BANK[c])
-            for d in range(CHUNKS):
-                nc.tensor.matmul_mx(
-                    out=y[c][:, block(d)],
-                    lhsT=h_code["b"][:, block(d)].bitcast(FP8X4),
-                    lhsT_scale=h_scale["b"][:, block(d)],
-                    rhs=h_code["a"][:, block(c)].bitcast(FP8X4),
-                    rhs_scale=h_scale["a"][:, block(c)],
-                    start=True,
-                    stop=True,
-                )
-
-        def plain_product(c):
-            y[c] = bank("y%d" % c, Y_BANK[c])
+        def y_pass(dst, still, moving):
             nc.tensor.matmul_mx(
-                out=y[c][:],
-                lhsT=h_code["a"][:, block(c)].bitcast(FP8X4),
-                lhsT_scale=h_scale["a"][:, block(c)],
-                rhs=h_code["b"][:].bitcast(FP8X4),
-                rhs_scale=h_scale["b"][:],
+                out=dst,
+                lhsT=h_code[still[0]][:, still[1]].bitcast(FP8X4),
+                lhsT_scale=h_scale[still[0]][:, still[1]],
+                rhs=h_code[moving[0]][:, moving[1]].bitcast(FP8X4),
+                rhs_scale=h_scale[moving[0]][:, moving[1]],
                 start=True,
                 stop=True,
             )
 
+        def turned_product(c, number):
+            y[c] = bank("y%d" % c, number)
+            for d in range(CHUNKS):
+                y_pass(y[c][:, block(d)], ("b", block(d)), ("a", block(c)))
+
+        def plain_product(c, number):
+            y[c] = bank("y%d" % c, number)
+            y_pass(y[c][:], ("a", block(c)), ("b", slice(0, V)))
+
+        def tanh_y(c, pieces):
+            half_tanh[c] = sb("half_tanh%d" % c, [P, V], F32)
+            for blocks in pieces:
+                nc.scalar.activation(half_tanh[c][:, columns(blocks)], y[c][:, columns(blocks)], TANH, scale=0.5)
+
         def finish_plain(c):
             diff = sb("diff", [P, V], F32)
             res = sb("res%d" % c, [P, V], F32)
-            halves = [slice(0, HALF), slice(HALF, V)]
-            for cols in halves:
+            for h in range(2):
                 nc.vector.scalar_tensor_tensor(
-                    diff[:, cols], half_tanh[c][:, cols], 0.5, sim_sb[:, c, cols], ALU.mult, ALU.subtract
+                    diff[:, half(h)], half_tanh[c][:, half(h)], 0.5, sim_sb[:, c, half(h)], ALU.mult, ALU.subtract
                 )
-            for cols in halves:
-                nc.vector.scalar_tensor_tensor(res[:, cols], diff[:, cols], 0.5, wt_sb[:, c, cols], ALU.add, ALU.mult)
+            for h in range(2):
+                nc.vector.scalar_tensor_tensor(res[:, half(h)], diff[:, half(h)], 0.5, wt_sb[:, c, half(h)], ALU.add, ALU.mult)
             nc.sync.dma_start(out[block(c), :], res[:])
 
-        def tanh_y(c):
-            half_tanh[c] = sb("half_tanh%d" % c, [P, V], F32)
-            for blocks in TANH_PIECES[c]:
-                nc.scalar.activation(half_tanh[c][:, columns(blocks)], y[c][:, columns(blocks)], TANH, scale=0.5)
+        def finish_turned(c, blocks):
+            cols = columns(blocks)
+            res = sb("res%d_%d" % (c, cols.start), [P, cols.stop - cols.start], F32)
+            nc.vector.scalar_tensor_tensor(res[:], total[c, blocks][:, cols], 0.5, wt_sb[:, c, cols], ALU.mult, ALU.mult)
+            nc.sync.dma_start(out[block(c), cols], res[:])
 
-        def finish(c):
-            for blocks, number in PIECES[c]:
-                cols = columns(blocks)
-                res = sb("res%d_%d" % (c, cols.start), [P, cols.stop - cols.start], F32)
-                nc.vector.scalar_tensor_tensor(
-                    res[:], total[c, blocks][:, cols], 0.5, wt_sb[:, c, cols], ALU.mult, ALU.mult
-                )
-                nc.sync.dma_start(out[block(c), cols], res[:])
-
-        turn_sim(B)
-        for c in (A, B):
-            chunk_product(1, "a", c, False)
-        turn_sim(C)
-        tanh_b()
-        for c in (C, D):
-            chunk_product(1, "a", c, True)
-            chunk_product(0, "a", c, False)
-        turn_sim(D)
-        tanh_a(A)
-        tanh_a(B)
+        whole = (0, 1, 2, 3)
+        turn_sim(B, 6)
+        half_product(1, "a", 0)
+        turn_sim(C, 7)
+        first_b = th_tile("b", 0, HALF)
+        for c in range(2):
+            tanh_chunk(first_b[:, :, block(c), :], "b", c)
+        tanh_half("b", 1)
+        for c, number in ((C, 0), (D, 6)):
+            chunk_product(1, "a", c, number)
+            chunk_product(0, "a", c)
+        turn_sim(D, 2)
+        tanh_half("a", 0)
         copy_sim(B)
         copy_sim(C)
-        open_total(B)
-        open_total(C)
-        tanh_a(C)
-        tanh_a(D)
+        open_total(B, whole, 3)
+        open_total(C, whole, 4)
+        for c in (C, D):
+            tanh_chunk(th_tile("a", P * c, P)[:], "a", c)
         copy_sim(D)
         for h in range(2):
-            scale_h("b", th_b[h], HALF * h, HALF)
-        scale_a(A)
-        scale_a(B)
+            scale_h("b", HALF * h, HALF)
+        scale_h("a", 0, HALF)
         quant_h("b", 0, ENTRIES)
         quant_h("a", 0, HALF)
-        plain_product(A)
-        second_product(B)
-        open_total(D)
-        tanh_y(A)
-        tanh_y(B)
-        scale_a(C)
-        scale_a(D)
-        quant_a(C)
-        quant_a(D)
-        second_product(C)
-        second_product(D)
-        close_total(B)
-        tanh_y(C)
-        tanh_y(D)
-        close_total(C)
-        close_total(D)
+        plain_product(A, 5)
+        turned_product(B, 1)
+        open_total(D, (0, 1, 2), 2)
+        open_total(D, (3,), 6)
+        tanh_y(A, [whole])
+        tanh_y(B, [whole])
+        for c in (C, D):
+            scale_h("a", P * c, P)
+        for c in (C, D):
+            quant_h("a", P * c, P)
+        turned_product(C, 7)
+        turned_product(D, 0)
+        close_total(B, whole)
+        tanh_y(C, [(0, 1), (2, 3)])
+        tanh_y(D, [(0, 1, 2), (3,)])
+        close_total(C, whole)
+        close_total(D, (0, 1, 2))
+        close_total(D, (3,))
         finish_plain(A)
-        for c in (B, C, D):
-            finish(c)
+        finish_turned(B, whole)
+        finish_turned(C, whole)
+        finish_turned(D, (0, 1, 2))
+        finish_turned(D, (3,))

@@ -203,9 +203,9 @@ def tile_picked_yhnet_grad_p_kernel(
             src = z[side, c][:].rearrange("p (pair e n) -> p pair n e", pair=2, e=2)
             nc.scalar.activation(dst, src, TANH, scale=2.0)
 
-        def tanh_half(side, h):
+        def tanh_half(side, h, pairs):
             dst = th_tile(side, HALF * h, HALF)
-            for pair in range(2):
+            for pair in pairs:
                 src = z[side, h, pair][:].rearrange("p (e n) -> p n e", e=2)
                 nc.scalar.activation(dst[:, pair], src, TANH, scale=2.0)
 
@@ -301,17 +301,17 @@ def tile_picked_yhnet_grad_p_kernel(
 
         whole = (0, 1, 2, 3)
         turn_sim(B, 6)
-        half_product(1, "a", 0)
         turn_sim(C, 7)
+        half_product(1, "a", 0)
         first_b = th_tile("b", 0, HALF)
         for c in range(2):
             tanh_chunk(first_b[:, :, block(c), :], "b", c)
-        tanh_half("b", 1)
+        tanh_half("b", 1, (1, 0))
         for c, number in ((C, 0), (D, 6)):
             chunk_product(1, "a", c, number)
             chunk_product(0, "a", c)
         turn_sim(D, 2)
-        tanh_half("a", 0)
+        tanh_half("a", 0, (0, 1))
         copy_sim(B)
         copy_sim(C)
         open_total(B, whole, 3)

from contextlib import ExitStack

import concourse.mybir as mybir

K, T, S, H, V = 1024, 2048, 512, 512, 512
FLOPS = 2 * K * H * (S + V) + 2 * H * S * V

F32 = mybir.dt.float32
BF16 = mybir.dt.bfloat16
I32 = mybir.dt.int32
U32 = mybir.dt.uint32
U16 = mybir.dt.uint16
U8 = mybir.dt.uint8
FP8X4 = mybir.dt.float8_e4m3fn_x4
ALU = mybir.AluOpType
TANH = mybir.ActivationFunctionType.Tanh
COPY = mybir.ActivationFunctionType.Copy

P = 128
PACK = 4
K_PASS = P * PACK
PASSES = K // K_PASS
ENTRIES = S
HALF = ENTRIES // 2
CHUNKS = ENTRIES // P
BANK = 512
QUADRANT = 32
SCALE_ROWS = 4
A, B, C, D = range(CHUNKS)


def tile_picked_yhnet_grad_p_kernel(
    tc, x_words, x_scales, w1, unit, inv, sim, wt, offs, other, out
):
    nc = tc.nc
    with ExitStack() as ctx:
        keep = ctx.enter_context(tc.tile_pool(name="keep", bufs=1))
        psum = ctx.enter_context(tc.psum_pool(name="psum", bufs=1))

        def sb(name, shape, dtype, tag=None):
            return keep.tile(shape, dtype, name=name, tag=tag or name, align_bytes=64)

        def bank(name, number):
            return psum.tile([P, BANK], F32, name=name, tag="bank%d" % number)

        def block(n):
            return slice(P * n, P * (n + 1))

        def half(h):
            return slice(HALF * h, HALF * (h + 1))

        def columns(blocks):
            return slice(P * blocks[0], P * (blocks[-1] + 1))

        lists = {side: keep.tile([P, ENTRIES // 16], U16, name="list_" + side) for side in ("b", "a")}
        word_table = [sb("word_table%d" % o, [P, T], U32) for o in range(PASSES)]
        scale_table = sb("scale_table", [P, T], U8)
        factor = {side: sb("factor_" + side, [P, PACK], F32) for side in ("b", "a")}

        nc.gpsimd.memset(scale_table[:].bitcast(I32), 0)
        ident = sb("ident", [P, P], F32)
        zeros = sb("zeros", [P, P], F32)
        nc.gpsimd.memset(zeros[:], 0.0)
        nc.gpsimd.affine_select(
            out=ident[:],
            in_=zeros[:],
            compare_op=ALU.not_equal,
            fill=1.0,
            base=0,
            pattern=[[-1, P]],
            channel_multiplier=1,
        )
        w_raw = [sb("w_raw%d" % o, [P, PACK, H], F32, tag="big%d" % o) for o in range(PASSES)]

        def load_words(o):
            nc.sync.dma_start(
                word_table[o][:].bitcast(I32),
                x_words[o].rearrange("p n j -> p (n j)").bitcast(I32),
            )

        def load_weights(o):
            rows = w1[K_PASS * o : K_PASS * (o + 1), :]
            nc.sync.dma_start(w_raw[o][:], rows.rearrange("(p j) c -> p j c", j=PACK))

        def load_scales(queue, rows):
            for r in rows:
                for o in range(PASSES):
                    queue.dma_start(
                        scale_table[SCALE_ROWS * o + r : P : QUADRANT, :].bitcast(I32),
                        x_scales[o, r : SCALE_ROWS * (P // QUADRANT) : SCALE_ROWS, :].bitcast(I32),
                    )

        load_words(0)
        nc.sync.dma_start(lists["b"][:], other)
        nc.sync.dma_start(lists["a"][:], offs)
        load_scales(nc.sync, (0, 1))
        load_weights(0)
        load_scales(nc.sync, (2, 3))
        load_weights(1)
        load_words(1)
        nc.sync.dma_start(factor["b"][:], inv.rearrange("(p s) one -> p (s one)", s=PACK))
        nc.sync.dma_start(factor["a"][:], unit.rearrange("(p s) one -> p (s one)", s=PACK))

        w_code = [sb("w_code%d" % o, [P, H], U32) for o in range(PASSES)]
        w_scale = [sb("w_scale%d" % o, [P, H], U8) for o in range(PASSES)]
        w_bf = {(o, pair): sb("w_bf%d%d" % (o, pair), [P, 2, K_PASS], BF16) for o in range(PASSES) for pair in range(2)}
        x_code = {(side, o): sb("x_code_%s%d" % (side, o), [P, ENTRIES], U32) for side in "ba" for o in range(PASSES)}
        x_scale = {"b": sb("x_scale_b", [P, ENTRIES], U8)}

        def gather_words(side, o, first, count):
            nc.vector.tensor_copy(
                x_code[side, o][:, first : first + count],
                word_table[o][:].indirect(lists[side][:, first // 16 : (first + count) // 16]),
            )

        def gather_scales(side):
            nc.vector.tensor_copy(x_scale[side][:], scale_table[:].indirect(lists[side][:]))

        def cast_w(o, pair, copy, first_m=0, count=P):
            ms = slice(first_m, first_m + count)
            src = w_raw[o][:].rearrange("p j (m pair e) -> p pair m j e", pair=2, e=2)[:, pair, ms]
            dst = w_bf[o, pair][:].rearrange("p e (m j) -> p m j e", j=PACK)[:, ms]
            copy(dst, src)

        def quant_w(o, pair):
            nc.vector.quantize_mx(
                out=w_code[o][:, half(pair)].bitcast(FP8X4),
                scales=w_scale[o][:, half(pair)],
                in_=w_bf[o, pair][:].rearrange("p e n -> p (e n)"),
            )

        def z_pass(dst, o, slot, side, cols, start, stop):
            nc.tensor.matmul_mx(
                out=dst,
                lhsT=w_code[o][:, block(slot)].bitcast(FP8X4),
                lhsT_scale=w_scale[o][:, block(slot)],
                rhs=x_code[side, o][:, cols].bitcast(FP8X4),
                rhs_scale=x_scale[side][SCALE_ROWS * o : P, cols],
                start=start,
                stop=stop,
            )

        z = {}

        def chunk_product(o, side, c, number=None):
            opens = number is not None
            if opens:
                z[side, c] = bank("z_%s%d" % (side, c), number)
            for slot in range(PACK):
                z_pass(z[side, c][:, block(slot)], o, slot, side, block(c), opens and slot == 0, not opens and slot == PACK - 1)

        def half_product(o, side, h, numbers=None):
            opens = numbers is not None
            for pair in range(2):
                if opens:
                    z[side, h, pair] = bank("z_%s%d%d" % (side, h, pair), numbers[pair])
                for e in range(2):
                    z_pass(z[side, h, pair][:, half(e)], o, 2 * pair + e, side, half(h), opens and e == 0, not opens and e == 1)

        for side in "ba":
            gather_words(side, 0, 0, ENTRIES)
        gather_scales("b")
        for pair in range(2):
            cast_w(0, pair, nc.scalar.copy)
        quant_w(0, 0)
        x_scale["a"] = sb("x_scale_a", [P, ENTRIES], U8, tag="w_bf00")
        gather_scales("a")
        quant_w(0, 1)
        chunk_product(0, "b", 0, 0)
        chunk_product(0, "b", 1, 1)
        half_product(0, "b", 1, (2, 3))
        half_product(0, "a", 0, (4, 5))
        cast_w(1, 0, nc.scalar.copy)
        cast_w(1, 1, nc.scalar.copy, 0, P // 2)
        cast_w(1, 1, nc.vector.tensor_copy, P // 2, P // 2)
        quant_w(1, 0)
        quant_w(1, 1)
        gather_words("b", 1, 0, P)
        gather_words("b", 1, P, P)
        gather_words("b", 1, HALF, HALF)
        gather_words("a", 1, 0, ENTRIES)
        chunk_product(1, "b", 0)
        chunk_product(1, "b", 1)
        half_product(1, "b", 1)

        sim_sb = sb("sim_sb", [P, CHUNKS, V], F32, tag="big0")
        wt_sb = sb("wt_sb", [P, CHUNKS, V], F32, tag="big1")
        for first, count in ((1, CHUNKS - 1), (0, 1)):
            rows = sim[P * first : P * (first + count), :]
            nc.sync.dma_start(sim_sb[:, first : first + count, :], rows.rearrange("(c p) v -> p c v", p=P))
        nc.sync.dma_start(wt_sb[:], wt.rearrange("(c p) v -> p c v", p=P))

        th = {}
        h_bf = {side: sb("h_bf_" + side, [P, ENTRIES, PACK], BF16) for side in "ab"}
        h_code = {side: sb("h_code_" + side, [P, ENTRIES], U32) for side in "ab"}
        h_scale = {side: sb("h_scale_" + side, [P, ENTRIES], U8) for side in "ab"}

        def th_tile(side, first, count):
            th[side, first] = sb("th_%s%d" % (side, first), [P, 2, count, 2], F32)
            return th[side, first]

        def tanh_chunk(dst, side, c):
            src = z[side, c][:].rearrange("p (pair e n) -> p pair n e", pair=2, e=2)
            nc.scalar.activation(dst, src, TANH, scale=2.0)

        def tanh_half(side, h, pairs):
            dst = th_tile(side, HALF * h, HALF)
            for pair in pairs:
                src = z[side, h, pair][:].rearrange("p (e n) -> p n e", e=2)
                nc.scalar.activation(dst[:, pair], src, TANH, scale=2.0)

        def scale_h(side, first, count):
            nc.vector.tensor_tensor(
                h_bf[side][:, first : first + count, :].rearrange("p n (pair e) -> p n pair e", e=2),
                th[side, first][:].rearrange("p pair n e -> p n pair e"),
                factor[side][:].rearrange("p (n pair e) -> p n pair e", n=1, e=2).to_broadcast([P, count, 2, 2]),
                ALU.mult,
            )

        def quant_h(side, first, count):
            nc.vector.quantize_mx(
                out=h_code[side][:, first : first + count].bitcast(FP8X4),
                scales=h_scale[side][:, first : first + count],
                in_=h_bf[side][:, first : first + count, :].rearrange("p n s -> p (n s)"),
            )

        half_tanh = {}
        sim_turned = {}
        sim_term = {}
        total = {}
        y = {}

        def turn_sim(c, number):
            sim_turned[c] = bank("sim_turned%d" % c, number)
            for d in range(CHUNKS):
                nc.tensor.transpose(sim_turned[c][:, block(d)], sim_sb[:, c, block(d)], ident[:])

        def copy_sim(c):
            sim_term[c] = sb("sim_term%d" % c, [P, V], F32)
            nc.scalar.activation(sim_term[c][:], sim_turned[c][:], COPY, bias=1.0, scale=-2.0)

        def add_turned(c, blocks, term, opens):
            for d in blocks:
                nc.tensor.matmul(
                    total[c, blocks][:, block(d)],
                    term[:, block(d)],
                    ident[:],
                    start=(opens and d == blocks[0]),
                    stop=(not opens and d == blocks[-1]),
                    is_transpose=True,
                )

        def open_total(c, blocks, number):
            total[c, blocks] = bank("total%d_%d" % (c, blocks[0]), number)
            add_turned(c, blocks, sim_term[c], True)

        def close_total(c, blocks):
            add_turned(c, blocks, half_tanh[c], False)

        def y_pass(dst, still, moving):
            nc.tensor.matmul_mx(
                out=dst,
                lhsT=h_code[still[0]][:, still[1]].bitcast(FP8X4),
                lhsT_scale=h_scale[still[0]][:, still[1]],
                rhs=h_code[moving[0]][:, moving[1]].bitcast(FP8X4),
                rhs_scale=h_scale[moving[0]][:, moving[1]],
                start=True,
                stop=True,
            )

        def turned_product(c, number):
            y[c] = bank("y%d" % c, number)
            for d in range(CHUNKS):
                y_pass(y[c][:, block(d)], ("b", block(d)), ("a", block(c)))

        def plain_product(c, number):
            y[c] = bank("y%d" % c, number)
            y_pass(y[c][:], ("a", block(c)), ("b", slice(0, V)))

        def tanh_y(c, pieces):
            half_tanh[c] = sb("half_tanh%d" % c, [P, V], F32)
            for blocks in pieces:
                nc.scalar.activation(half_tanh[c][:, columns(blocks)], y[c][:, columns(blocks)], TANH, scale=0.5)

        def finish_plain(c):
            diff = sb("diff", [P, V], F32)
            res = sb("res%d" % c, [P, V], F32)
            for h in range(2):
                nc.vector.scalar_tensor_tensor(
                    diff[:, half(h)], half_tanh[c][:, half(h)], 0.5, sim_sb[:, c, half(h)], ALU.mult, ALU.subtract
                )
            for h in range(2):
                nc.vector.scalar_tensor_tensor(res[:, half(h)], diff[:, half(h)], 0.5, wt_sb[:, c, half(h)], ALU.add, ALU.mult)
            nc.sync.dma_start(out[block(c), :], res[:])

        def finish_turned(c, blocks):
            cols = columns(blocks)
            res = sb("res%d_%d" % (c, cols.start), [P, cols.stop - cols.start], F32)
            nc.vector.scalar_tensor_tensor(res[:], total[c, blocks][:, cols], 0.5, wt_sb[:, c, cols], ALU.mult, ALU.mult)
            nc.sync.dma_start(out[block(c), cols], res[:])

        whole = (0, 1, 2, 3)
        turn_sim(B, 6)
        turn_sim(C, 7)
        half_product(1, "a", 0)
        first_b = th_tile("b", 0, HALF)
        for c in range(2):
            tanh_chunk(first_b[:, :, block(c), :], "b", c)
        tanh_half("b", 1, (1, 0))
        for c, number in ((C, 0), (D, 6)):
            chunk_product(1, "a", c, number)
            chunk_product(0, "a", c)
        turn_sim(D, 2)
        tanh_half("a", 0, (0, 1))
        copy_sim(B)
        copy_sim(C)
        open_total(B, whole, 3)
        open_total(C, whole, 4)
        for c in (C, D):
            tanh_chunk(th_tile("a", P * c, P)[:], "a", c)
        copy_sim(D)
        for h in range(2):
            scale_h("b", HALF * h, HALF)
        scale_h("a", 0, HALF)
        quant_h("b", 0, ENTRIES)
        quant_h("a", 0, HALF)
        plain_product(A, 5)
        turned_product(B, 1)
        open_total(D, (0, 1, 2), 2)
        open_total(D, (3,), 6)
        tanh_y(A, [whole])
        tanh_y(B, [whole])
        for c in (C, D):
            scale_h("a", P * c, P)
        for c in (C, D):
            quant_h("a", P * c, P)
        turned_product(C, 7)
        turned_product(D, 0)
        close_total(B, whole)
        tanh_y(C, [(0, 1), (2, 3)])
        tanh_y(D, [(0, 1, 2), (3,)])
        close_total(C, whole)
        close_total(D, (0, 1, 2))
        close_total(D, (3,))
        finish_plain(A)
        finish_turned(B, whole)
        finish_turned(C, whole)
        finish_turned(D, (0, 1, 2))
        finish_turned(D, (3,))
